import numpy as np
import ml_dtypes


def mxq(x, axis, fmt="e4m3"):
    dtype, down = {"e4m3": (ml_dtypes.float8_e4m3fn, 7), "e5m2": (ml_dtypes.float8_e5m2, 14)}[fmt]
    v = np.moveaxis(np.asarray(x, np.float32).astype(ml_dtypes.bfloat16).astype(np.float64), axis, -1)
    blocks = v.reshape(v.shape[:-1] + (-1, 32))
    amax = np.abs(blocks).max(-1, keepdims=True)
    byte = np.maximum(np.where(amax > 0, np.frexp(amax)[1] - 1 + 127, 0) - down, 1)
    scale = np.exp2(byte - 127.0)
    codes = (blocks / scale).astype(np.float32).astype(dtype).astype(np.float64)
    return np.moveaxis((codes * scale).reshape(v.shape), -1, axis)


WIDE = False


def mx_kscale(k):
    if not WIDE:
        return np.ones(k)
    levels = np.array([10, -10, 5, -5, 0])
    if k % 512:
        return np.exp2(np.random.permutation(np.resize(levels, k // 32))).repeat(32)
    a = np.empty((k // 512, 16))
    for p in range(k // 512):
        a[p, :8] = np.random.permutation(np.resize(levels, 8))
        for g in range(8):
            far = levels[np.abs(levels - a[p, g]) >= 10]
            a[p, g + 8] = far[np.random.randint(len(far))]
    return np.exp2(a.ravel()).repeat(32)


BF16 = ml_dtypes.bfloat16


def bf(x):
    return np.asarray(x, np.float32).astype(BF16)


def f64(x):
    return np.asarray(x).astype(np.float64)


E2M1 = np.array([0.0, 0.5, 1.0, 1.5, 2.0, 3.0, 4.0, 6.0, -0.0, -0.5, -1.0, -1.5, -2.0, -3.0, -4.0, -6.0])


def pack_weight(w, fmt):
    k, n = w.shape
    w = f64(bf(w)).reshape(k // 32, 32, n)
    amax = np.abs(w).max(1)
    if fmt == "e4m3":
        byte = np.frexp(amax)[1] - 1 + 127 - 7
    else:
        mant, ex = np.frexp(amax / 6.0)
        byte = np.where(mant > 0.5, ex, ex - 1) + 127
    byte = np.clip(np.where(amax > 0, byte, 1), 1, 254)
    scaled = (w * np.exp2(127.0 - byte)[:, None, :]).reshape(k, n).astype(np.float32)
    by_word = np.ascontiguousarray(scaled.reshape(k // 512, 128, 4, n).transpose(0, 1, 3, 2))
    if fmt == "e4m3":
        words = by_word.astype(ml_dtypes.float8_e4m3fn).view(np.uint8)
    else:
        c = by_word.astype(ml_dtypes.float4_e2m1fn).view(np.uint8) & 0xF
        words = c[..., 0::2] | (c[..., 1::2] << 4)
    return np.ascontiguousarray(words), np.ascontiguousarray(byte.astype(np.uint8).reshape(k // 512, 16, n))


def unpack_weight(words, scales, fmt):
    g, p, n, _ = words.shape
    if fmt == "e4m3":
        vals = np.ascontiguousarray(words).view(ml_dtypes.float8_e4m3fn).astype(np.float64)
    else:
        nib = np.empty((g, p, n, 4), np.uint8)
        nib[..., 0::2] = words & 0xF
        nib[..., 1::2] = words >> 4
        vals = E2M1[nib]
    vals = vals * np.repeat(np.exp2(scales.astype(np.float64) - 127.0), 8, axis=1)[..., None]
    return vals.transpose(0, 1, 3, 2).reshape(g * 512, n)
def pack4(w):
    words, scales = pack_weight(w, "e2m1")
    return words.reshape(words.shape[0], 128, -1), scales


def unpack4(words, scales):
    return unpack_weight(words.reshape(words.shape[0], 128, -1, 2), scales, "e2m1")


B, D, E, Q = 1024, 1024, 1024, 1024


def huber_influence(r):
    return np.maximum(-1.0, np.minimum(1.0, r))


def draw0():
    s = mx_kscale(D)
    u = mx_kscale(B)
    x = bf(np.random.standard_normal((B, D)) * s)
    m_words, m_scales = pack4(np.random.standard_normal((D, E)) / np.sqrt(D) / s[:, None])
    return {"x": x,
            "m_words": m_words,
            "m_scales": m_scales,
            "b": bf(0.5 * np.random.standard_normal(E)),
            "y": bf(np.random.standard_normal((B, E))),
            "c": bf((1.0 + 0.1 * np.random.standard_normal(B)) * u),
            "z": bf(np.random.standard_normal((B, Q)) / u[:, None])}


def core(x, m_words, m_scales, b, y, c, z):
    n = x.shape[0]
    r = (mxq(f64(x), 1, "e4m3") @ unpack4(m_words, m_scales)) + f64(b) - f64(y)
    psi = huber_influence(r)
    t = f64(c)[:, None] * psi
    return (mxq(f64(z), 0, "e4m3").T @ mxq(t, 0, "e4m3")) / np.sqrt(n)


def e4m3fn_bytes(y):
    return np.clip(np.asarray(y, np.float64), -448.0, 448.0).astype(np.float32).astype(ml_dtypes.float8_e4m3fn).view(np.uint8)


def e4m3fn_values(b):
    return np.asarray(b, np.uint8).view(ml_dtypes.float8_e4m3fn).astype(np.float64)


def setup_inputs():
    d = draw0()
    x0 = np.asarray(d['z']).astype(np.float64)
    s = (np.max(np.abs(x0), axis=(1,), keepdims=True) / 448.0).astype(np.float32)
    out = {}
    for k, v in d.items():
        if k == 'z':
            out['z_bytes'] = e4m3fn_bytes(x0 / s.astype(np.float64))
            out['z_scale'] = s
        else:
            out[k] = v
    return out


def reference(x, m_words, m_scales, b, y, c, z_bytes, z_scale):
    return core(x, m_words, m_scales, b, y, c, e4m3fn_values(z_bytes) * z_scale.astype(np.float64))

@@ -1,0 +1,492 @@
+import math
+from contextlib import ExitStack
+
+import concourse.mybir as mybir
+from concourse.masks import make_identity
+
+B, D, E, Q = 1024, 1024, 1024, 1024
+FLOPS = 2 * B * D * E + 2 * B * Q * E
+
+F32 = mybir.dt.float32
+BF16 = mybir.dt.bfloat16
+I32 = mybir.dt.int32
+U32 = mybir.dt.uint32
+U8 = mybir.dt.uint8
+FP8 = mybir.dt.float8_e4m3fn
+FP8X4 = mybir.dt.float8_e4m3fn_x4
+FP4X4 = mybir.dt.float4_e2m1fn_x4
+ALU = mybir.AluOpType
+COPY = mybir.ActivationFunctionType.Copy
+
+P = 128
+PACK = 4
+PASSES = 2
+BANK = 512
+CHUNKS = ((0, 512), (512, 256), (768, 256))
+Z_COLS = 512
+OUT_SCALE = 1.0 / math.sqrt(B)
+
+TURN_BANKS = (0, 1, 6, 7)
+ACC_BANKS = (2, 3)
+W_BANKS = (4, 5)
+TS = (10,)
+ZQ = (1, 6, 9)
+CY = (3, 6, 7, 11)
+WJ = (0, 1, 2, 4, 4, 4, 7, 8)
+OJ = (0, 2, 4, 6, 8, 8, 10, 12)
+
+
+def tile_iv4rechubermomentmatrix_w4_kernel(tc, x, m_words, m_scales, b, y, c, z_bytes, z_scale, out):
+    nc = tc.nc
+
+    steps = []
+    for ch, (e0, width) in enumerate(CHUNKS):
+        per_bank = BANK // width
+        for g in range(PASSES):
+            for j0 in range(0, PACK, per_bank):
+                steps.append((ch, g, range(j0, j0 + per_bank)))
+    n_steps = len(steps)
+    n_slots = PASSES * PACK
+    wide_steps = PASSES * PACK
+    z_pieces = [(g, h) for h in range(Q // Z_COLS) for g in range(PASSES)]
+
+    def on_vector(s):
+        return s >= wide_steps and s % 2 == 1
+
+    x_rows = x.rearrange("(g p j) d -> g j p d", p=P, j=PACK)
+    y_rows = y.rearrange("(g p j) e -> g p j e", p=P, j=PACK)
+    z_rows = z_bytes.rearrange("(g p j) q -> g p j q", p=P, j=PACK)
+    out_rows = out.rearrange("(k p) e -> p k e", p=P)
+
+    with ExitStack() as ctx:
+        keep = ctx.enter_context(tc.tile_pool(name="keep", bufs=1))
+        ring = ctx.enter_context(tc.tile_pool(name="ring", bufs=4))
+        psum = ctx.enter_context(tc.psum_pool(name="psum", bufs=1))
+        ctx.enter_context(tc.manual_schedule())
+
+        def kept(name, shape, dtype):
+            return keep.tile(shape, dtype, name=name, align_bytes=64)
+
+        def bank(index):
+            return psum.tile([P, BANK], F32, name="bank%d" % index)
+
+        m_scale = kept("m_scale", [P, PASSES, E], U8)
+        b_row = kept("b_row", [P, E], BF16)
+        ident32 = kept("ident32", [P, P], F32)
+        ident16 = kept("ident16", [P, P], BF16)
+        minus_ones = kept("minus_ones", [P, P], BF16)
+        zs = kept("zs", [P, PASSES, PACK], F32)
+        c16 = kept("c16", [P, PASSES, PACK], BF16)
+        c32 = kept("c32", [P, PASSES, PACK], F32)
+        c_hi = kept("c_hi", [P, PASSES, PACK], F32)
+        c_lo = kept("c_lo", [P, PASSES, PACK], F32)
+        minus_b = kept("minus_b", [P, BANK], F32)
+
+        x_in = [kept("x_in%d" % i, [P, D], BF16) for i in range(n_slots)]
+        y_in = [kept("y_in%d" % i, [P, 2 * BANK], BF16) for i in range(n_steps // 2)]
+        z_in = [kept("z_in%d" % i, [P, PACK, Z_COLS], U8) for i in range(len(z_pieces))]
+        m_in = [kept("m_in%d" % ch, [P, PASSES, 2 * w], U8) for ch, (e0, w) in enumerate(CHUNKS)]
+
+        def load_x(i):
+            nc.sync.dma_start(out=x_in[i][:], in_=x_rows[i // PACK, i % PACK])
+
+        def load_y(i):
+            ch, g, js = steps[2 * i]
+            e0, w = CHUNKS[ch]
+            planes = 2 * BANK // w
+            nc.sync.dma_start(
+                out=y_in[i][:].rearrange("p (j e) -> p j e", j=planes),
+                in_=y_rows[g][:, js[0] : js[0] + planes, e0 : e0 + w],
+            )
+
+        def load_z(i):
+            g, h = z_pieces[i]
+            nc.sync.dma_start(out=z_in[i][:], in_=z_rows[g][:, :, h * Z_COLS : (h + 1) * Z_COLS])
+
+        def load_m(ch):
+            e0, w = CHUNKS[ch]
+            nc.sync.dma_start(
+                out=m_in[ch][:].bitcast(I32),
+                in_=m_words.rearrange("g p n -> p g n")[:, :, 2 * e0 : 2 * (e0 + w)].bitcast(I32),
+            )
+
+        nc.vector.memset(b_row[:].bitcast(I32), 0)
+        nc.vector.memset(m_scale[:].rearrange("p g n -> p (g n)").bitcast(I32), 0)
+        make_identity(nc, ident32[:])
+        nc.gpsimd.memset(minus_ones[:], -1.0)
+
+        nc.sync.dma_start(out=zs[:], in_=z_scale.rearrange("(g p j) o -> p g (j o)", p=P, j=PACK))
+        nc.sync.dma_start(out=c16[:], in_=c.rearrange("(g p j) -> p g j", p=P, j=PACK))
+        load_z(0)
+        load_x(0)
+        load_x(1)
+        load_m(0)
+        nc.scalar.dma_start(out=b_row[0:1, :], in_=b.rearrange("(o e) -> o e", o=1))
+        for quad in range(4):
+            nc.sync.dma_start(
+                out=m_scale[32 * quad : 32 * quad + 4].bitcast(I32),
+                in_=m_scales[:, 4 * quad : 4 * quad + 4, :].rearrange("g r n -> r g n").bitcast(I32),
+            )
+        load_y(0)
+        load_z(1)
+        load_x(2)
+        load_x(3)
+        load_z(2)
+        load_y(1)
+        load_x(4)
+        load_x(5)
+        load_z(3)
+        load_y(2)
+        load_x(6)
+        load_x(7)
+        load_y(4)
+        load_y(3)
+        load_m(1)
+        load_y(5)
+        load_m(2)
+        load_y(6)
+        load_y(7)
+        nc.scalar.copy(out=ident16[:], in_=ident32[:])
+
+        x_turned = {}
+        x_grouped = {}
+        x_q = {}
+        z_wide = {}
+        z_grouped = {}
+        z_q = {}
+        w_bank = {}
+        cw = {}
+        acc = {}
+        pre = {}
+        t_planes = {}
+        t_grouped = {}
+        t_q = {}
+        out_bank = {}
+
+        def quantize(name, grouped, cols):
+            codes = kept(name + "_codes", [P, cols], U32)
+            scales = kept(name + "_scales", [P, cols], U8)
+            nc.vector.quantize_mx(out=codes[:].bitcast(FP8X4), scales=scales[:], in_=grouped[:])
+            return codes, scales
+
+        def interleave(engine, grouped, planes):
+            dst = grouped.rearrange("p (n i j) -> p n j i", i=4, j=PACK)
+            src = planes.rearrange("p j (n i) -> p n j i", i=4)
+            if engine == "vector":
+                nc.vector.tensor_copy(out=dst, in_=src)
+            else:
+                nc.scalar.copy(out=dst, in_=src)
+
+        def turn_x(i):
+            x_turned[i] = bank(TURN_BANKS[i % 4])
+            words = x_in[i][:].bitcast(F32)
+            for kp in range(PASSES):
+                for u in range(2):
+                    col = (2 * kp + u) * P
+                    nc.tensor.transpose(
+                        x_turned[i][:, col : col + P], words[:, 256 * kp + u : 256 * (kp + 1) : 2], ident32[:]
+                    )
+
+        def copy_x(i):
+            x_grouped[i] = ring.tile([P, D], BF16, name="x_grouped", align_bytes=64)
+            nc.scalar.copy(
+                out=x_grouped[i][:].bitcast(F32).rearrange("p (k r u) -> p k r u", k=PASSES, u=2),
+                in_=x_turned[i][:].rearrange("p (k u r) -> p k r u", k=PASSES, u=2),
+            )
+
+        def quantize_x(i):
+            x_q[i] = quantize("x%d" % i, x_grouped[i], PASSES * P)
+
+        def widen_z(i, j, engine):
+            g, h = z_pieces[i]
+            if i not in z_wide:
+                z_wide[i] = kept("z_wide%d" % i, [P, PACK, Z_COLS], BF16)
+            src = z_in[i][:, j, :].bitcast(FP8)
+            if engine == "vector":
+                nc.vector.tensor_scalar(
+                    out=z_wide[i][:, j, :], in0=src, scalar1=zs[:, g, j : j + 1], scalar2=None, op0=ALU.mult
+                )
+            else:
+                nc.scalar.activation(out=z_wide[i][:, j, :], in_=src, func=COPY, scale=zs[:, g, j : j + 1])
+
+        def group_z(i, engine, half):
+            if i not in z_grouped:
+                z_grouped[i] = kept("z_grouped%d" % i, [P, PACK * Z_COLS], BF16)
+            cols = slice(0, Z_COLS) if half is None else slice(half * Z_COLS // 2, (half + 1) * Z_COLS // 2)
+            interleave(engine, z_grouped[i][:, PACK * cols.start : PACK * cols.stop], z_wide[i][:, :, cols])
+
+        def quantize_z(i):
+            z_q[z_pieces[i]] = quantize("z%d" % i, z_grouped[i], Z_COLS)
+
+        def y_plane(s, jj):
+            w = CHUNKS[steps[s][0]][1]
+            col = (s % 2) * BANK + jj * w
+            return y_in[s // 2][:, col : col + w]
+
+        def spread_b():
+            spread = bank(TURN_BANKS[3])
+            nc.tensor.matmul(spread[:], lhsT=minus_ones[:], rhs=b_row[:, BANK:], start=True, stop=True)
+            w_bank["b"] = spread
+
+        def copy_b():
+            nc.scalar.copy(out=minus_b[:], in_=w_bank["b"][:])
+
+        def open_w(s):
+            ch, g, js = steps[s]
+            e0, w = CHUNKS[ch]
+            w_bank[s] = bank(W_BANKS[s % 2])
+            nc.tensor.matmul(w_bank[s][:], lhsT=minus_ones[:], rhs=b_row[:, e0 : e0 + w], start=True, stop=False)
+
+        def close_w(s):
+            nc.tensor.matmul(w_bank[s][:], lhsT=ident16[:], rhs=y_plane(s, 0), start=False, stop=True)
+
+        def y_minus_b(s):
+            ch, g, js = steps[s]
+            e0, w = CHUNKS[ch]
+            if on_vector(s):
+                return
+            w_bank[s] = bank(W_BANKS[s % 2] if s < wide_steps else W_BANKS[s // 2 % 2])
+            for jj in range(len(js)):
+                dst = w_bank[s][:, jj * w : (jj + 1) * w]
+                nc.tensor.matmul(dst, lhsT=minus_ones[:], rhs=b_row[:, e0 : e0 + w], start=True, stop=False)
+                nc.tensor.matmul(dst, lhsT=ident16[:], rhs=y_plane(s, jj), start=False, stop=True)
+
+        def scale_w(s):
+            ch, g, js = steps[s]
+            e0, w = CHUNKS[ch]
+            if on_vector(s):
+                cw[s] = kept("minus_cb%d" % s, [P, BANK], F32)
+            else:
+                cw[s] = ring.tile([P, BANK], F32, name="cw", align_bytes=64)
+            for jj, j in enumerate(js):
+                cols = slice(jj * w, (jj + 1) * w)
+                src = minus_b[:, e0 - BANK : e0 - BANK + w] if on_vector(s) else w_bank[s][:, cols]
+                nc.scalar.activation(out=cw[s][:, cols], in_=src, func=COPY, scale=c32[:, g, j : j + 1])
+
+        def add_cy(s):
+            ch, g, js = steps[s]
+            e0, w = CHUNKS[ch]
+            if not on_vector(s):
+                return
+            minus_cb = cw[s]
+            cw[s] = ring.tile([P, BANK], F32, name="cw_sum", align_bytes=64)
+            for jj, j in enumerate(js):
+                cols = slice(jj * w, (jj + 1) * w)
+                nc.vector.scalar_tensor_tensor(
+                    out=cw[s][:, cols], in0=y_plane(s, jj), scalar=c32[:, g, j : j + 1], in1=minus_cb[:, cols],
+                    op0=ALU.mult, op1=ALU.add,
+                )
+
+        def first_product(s):
+            ch, g, js = steps[s]
+            e0, w = CHUNKS[ch]
+            n = w if w == BANK else P
+            acc[s] = bank(ACC_BANKS[s % 2])
+            for jj, j in enumerate(js):
+                codes, scales = x_q[g * PACK + j]
+                for n0 in range(0, w, n):
+                    for kp in range(PASSES):
+                        nc.tensor.matmul_mx(
+                            out=acc[s][:, jj * w + n0 : jj * w + n0 + n],
+                            lhsT=codes[:, kp * P : (kp + 1) * P].bitcast(FP8X4),
+                            lhsT_scale=scales[:, kp * P : (kp + 1) * P],
+                            rhs=m_in[ch][:, kp, 2 * n0 : 2 * (n0 + n)].bitcast(FP4X4),
+                            rhs_scale=m_scale[:, kp, e0 + n0 : e0 + n0 + n],
+                            start=(kp == 0),
+                            stop=(kp == PASSES - 1),
+                        )
+
+        def residual(s):
+            ch, g, js = steps[s]
+            e0, w = CHUNKS[ch]
+            pre[s] = ring.tile([P, BANK], F32, name="pre", align_bytes=64)
+            for jj, j in enumerate(js):
+                cols = slice(jj * w, (jj + 1) * w)
+                nc.vector.scalar_tensor_tensor(
+                    out=pre[s][:, cols], in0=acc[s][:, cols], scalar=c32[:, g, j : j + 1], in1=cw[s][:, cols],
+                    op0=ALU.mult, op1=ALU.subtract,
+                )
+
+        def clip(s, only=None):
+            ch, g, js = steps[s]
+            e0, w = CHUNKS[ch]
+            if (ch, g) not in t_planes:
+                t_planes[ch, g] = kept("t_planes%d_%d" % (ch, g), [P, PACK, w], BF16)
+            for jj, j in enumerate(js):
+                if (only is not None and jj != only) or (only is None and s == 8 and jj == 0):
+                    continue
+                nc.vector.tensor_scalar(
+                    out=t_planes[ch, g][:, j, :], in0=pre[s][:, jj * w : (jj + 1) * w],
+                    scalar1=c_hi[:, g, j : j + 1], scalar2=c_lo[:, g, j : j + 1], op0=ALU.min, op1=ALU.max,
+                )
+
+        def closes_group(s):
+            return steps[s][2][-1] == PACK - 1
+
+        def group_t(s, engine):
+            ch, g, js = steps[s]
+            t_grouped[ch, g] = kept("t_grouped%d_%d" % (ch, g), [P, PACK * CHUNKS[ch][1]], BF16)
+            interleave(engine, t_grouped[ch, g][:], t_planes[ch, g][:])
+
+        def quantize_t(s):
+            ch, g, js = steps[s]
+            t_q[ch, g] = quantize("t%d_%d" % (ch, g), t_grouped[ch, g], CHUNKS[ch][1])
+
+        def second_pass(ch, k, g, dst):
+            z_codes, z_scales = z_q[g, k * P // Z_COLS]
+            t_codes, t_scales = t_q[ch, g]
+            q0 = k * P % Z_COLS
+            nc.tensor.matmul_mx(
+                out=dst,
+                lhsT=z_codes[:, q0 : q0 + P].bitcast(FP8X4),
+                lhsT_scale=z_scales[:, q0 : q0 + P],
+                rhs=t_codes[:].bitcast(FP8X4),
+                rhs_scale=t_scales[:],
+                start=(g == 0),
+                stop=(g == PASSES - 1),
+            )
+
+        def second_product(ch, i):
+            w = CHUNKS[ch][1]
+            per_bank = BANK // w
+            out_bank[ch, i] = bank(TURN_BANKS[i % 4])
+            for kk in range(per_bank):
+                for g in range(PASSES):
+                    second_pass(ch, i * per_bank + kk, g, out_bank[ch, i][:, kk * w : (kk + 1) * w])
+
+        def open_out(i):
+            out_bank[0, i] = bank(TURN_BANKS[i])
+            second_pass(0, i, 0, out_bank[0, i][:])
+
+        def close_out(i):
+            second_pass(0, i, 1, out_bank[0, i][:])
+
+        def store(ch, src, k0, blocks, engine):
+            e0, w = CHUNKS[ch]
+            result = keep.tile([P, blocks * w], F32, name="result%d_%d" % (ch, k0), align_bytes=64)
+            if engine == "vector":
+                nc.vector.tensor_scalar(out=result[:], in0=src, scalar1=OUT_SCALE, scalar2=None, op0=ALU.mult)
+            else:
+                nc.scalar.activation(out=result[:], in_=src, func=COPY, scale=OUT_SCALE)
+            nc.sync.dma_start(
+                out=out_rows[:, k0 : k0 + blocks, e0 : e0 + w], in_=result[:].rearrange("p (k e) -> p k e", k=blocks)
+            )
+
+        def store_bank(ch, i):
+            per_bank = BANK // CHUNKS[ch][1]
+            store(ch, out_bank[ch, i][:], i * per_bank, per_bank, "scalar")
+
+        for j in range(3):
+            widen_z(0, j, "vector")
+        widen_z(0, 3, "scalar")
+        nc.vector.tensor_copy(out=c32[:], in_=c16[:])
+        nc.vector.scalar_tensor_tensor(out=c_hi[:], in0=c16[:], scalar=-1.0, in1=c16[:], op0=ALU.mult, op1=ALU.max)
+        nc.vector.scalar_tensor_tensor(out=c_lo[:], in0=c16[:], scalar=-1.0, in1=c16[:], op0=ALU.mult, op1=ALU.min)
+        turn_x(0)
+        spread_b()
+        open_w(0)
+        copy_x(0)
+        copy_b()
+        turn_x(1)
+        copy_x(1)
+        open_w(1)
+        group_z(0, "vector", None)
+        quantize_x(0)
+        quantize_z(0)
+        quantize_x(1)
+        scale_w(9)
+        scale_w(11)
+        scale_w(13)
+        close_w(0)
+        scale_w(0)
+        scale_w(15)
+        for j in range(PACK):
+            widen_z(1, j, "vector")
+
+        widen_jobs = [(i, j) for i in range(2, len(z_pieces)) for j in range(PACK)]
+        for s in range(n_steps + 1):
+            if 1 <= s < wide_steps:
+                y_minus_b(s + 1)
+            elif s >= wide_steps and s + 2 < n_steps:
+                y_minus_b(s + 2)
+            if s < n_steps:
+                first_product(s)
+            if s == 0:
+                close_w(1)
+            if s in (0, 1, 3):
+                turn_x(s + 2 + s % 2)
+                turn_x(s + 3 + s % 2)
+            if s in (6, 7):
+                open_out(2 * (s - 6))
+                open_out(2 * (s - 6) + 1)
+            if s == 10:
+                for i in range(4):
+                    close_out(i)
+            if s in (11, 12):
+                second_product(0, 2 * s - 18)
+                second_product(0, 2 * s - 17)
+            if s in (14, 15):
+                second_product(1, 2 * s - 28)
+                second_product(1, 2 * s - 27)
+            if s < wide_steps:
+                scale_w(s + 1)
+            elif s + 2 < n_steps and not on_vector(s + 2):
+                scale_w(s + 2)
+            if s < 2:
+                copy_x(2 * s + 2)
+                copy_x(2 * s + 3)
+            if s in (3, 4):
+                copy_x(s + 3)
+            for i, j in widen_jobs[WJ[min(s, 7)] : WJ[min(s + 1, 7)]]:
+                widen_z(i, j, "scalar")
+            if s in (3, 4):
+                group_z(2, "scalar", s - 3)
+            if s == 7:
+                group_z(3, "scalar", 0)
+                group_z(3, "scalar", 1)
+            if s == 10:
+                for i in range(3):
+                    store_bank(0, i)
+            if s in CY:
+                add_cy(9 + 2 * CY.index(s))
+            if s == 1:
+                quantize_x(2)
+            if 2 <= s and s + 2 < n_slots:
+                quantize_x(s + 2)
+            if s >= 1:
+                clip(s - 1)
+            if s < n_steps:
+                residual(s)
+            if s == 1:
+                quantize_x(3)
+            if s in ZQ:
+                quantize_z(ZQ.index(s) + 1)
+            if s == 0:
+                group_z(1, "vector", None)
+            if s >= 1 and closes_group(s - 1):
+                group_t(s - 1, "scalar" if s in TS else "vector")
+            if s >= 2 and closes_group(s - 2) and s != 9:
+                quantize_t(s - 2)
+            if s == 8:
+                clip(8, 0)
+                quantize_t(7)
+            if s == 10:
+                store_bank(0, 3)
+            if s in (11, 12):
+                store_bank(0, 2 * s - 18)
+                store_bank(0, 2 * s - 17)
+            if s in (14, 15):
+                store_bank(1, 2 * s - 28)
+                store_bank(1, 2 * s - 27)
+            if s == n_steps:
+                last = len(CHUNKS) - 1
+                w = CHUNKS[last][1]
+                order = W_BANKS + TURN_BANKS + ACC_BANKS
+                for k in range(Q // P):
+                    out_bank[last, k] = bank(order[k])
+                    second_pass(last, k, 0, out_bank[last, k][:, :w])
+
+        quantize_t(n_steps - 1)
+        for k in range(Q // P):
+            second_pass(last, k, 1, out_bank[last, k][:, :w])
+            store(last, out_bank[last, k][:, :w], k, 1, "scalar" if k % 2 == 0 else "vector")

@@ -26,12 +26,16 @@ CHUNKS = ((0, 512), (512, 256), (768, 256))
 Z_COLS = 512
 OUT_SCALE = 1.0 / math.sqrt(B)
 
-TURN_BANKS = (0, 1, 6, 7)
-ACC_BANKS = (2, 3)
-W_BANKS = (4, 5)
-TS = (10,)
+ACC_BANKS = (2, 3, 6, 7)
+SIDE_BANKS = (0, 1, 4, 5)
+TS = ()
+VS = (0, 1, 2, 3)
+GS = 6
+ZV = 3
+REST = "vector"
+Z1V = 4
+ZG = {(1, None): (0, "vector"), (2, 0): (3, "scalar"), (2, 1): (4, "scalar"), (3, 0): (7, "scalar"), (3, 1): (7, "scalar")}
 ZQ = (1, 6, 9)
-CY = (3, 6, 7, 11)
 WJ = (0, 1, 2, 4, 4, 4, 7, 8)
 OJ = (0, 2, 4, 6, 8, 8, 10, 12)
 
@@ -50,9 +54,6 @@ def tile_iv4rechubermomentmatrix_w4_kernel(tc, x, m_words, m_scales, b, y, c, z_
     wide_steps = PASSES * PACK
     z_pieces = [(g, h) for h in range(Q // Z_COLS) for g in range(PASSES)]
 
-    def on_vector(s):
-        return s >= wide_steps and s % 2 == 1
-
     x_rows = x.rearrange("(g p j) d -> g j p d", p=P, j=PACK)
     y_rows = y.rearrange("(g p j) e -> g p j e", p=P, j=PACK)
     z_rows = z_bytes.rearrange("(g p j) q -> g p j q", p=P, j=PACK)
@@ -61,8 +62,15 @@ def tile_iv4rechubermomentmatrix_w4_kernel(tc, x, m_words, m_scales, b, y, c, z_
     with ExitStack() as ctx:
         keep = ctx.enter_context(tc.tile_pool(name="keep", bufs=1))
         ring = ctx.enter_context(tc.tile_pool(name="ring", bufs=4))
+        deep = ctx.enter_context(tc.tile_pool(name="deep", bufs=8))
         psum = ctx.enter_context(tc.psum_pool(name="psum", bufs=1))
         ctx.enter_context(tc.manual_schedule())
+
+        side_uses = []
+
+        def side_bank():
+            side_uses.append(None)
+            return bank(SIDE_BANKS[(len(side_uses) - 1) % len(SIDE_BANKS)])
 
         def kept(name, shape, dtype):
             return keep.tile(shape, dtype, name=name, align_bytes=64)
@@ -115,10 +123,10 @@ def tile_iv4rechubermomentmatrix_w4_kernel(tc, x, m_words, m_scales, b, y, c, z_
         make_identity(nc, ident32[:])
         nc.gpsimd.memset(minus_ones[:], -1.0)
 
-        nc.sync.dma_start(out=zs[:], in_=z_scale.rearrange("(g p j) o -> p g (j o)", p=P, j=PACK))
-        nc.sync.dma_start(out=c16[:], in_=c.rearrange("(g p j) -> p g j", p=P, j=PACK))
         load_z(0)
+        nc.scalar.dma_start(out=zs[:], in_=z_scale.rearrange("(g p j) o -> p g (j o)", p=P, j=PACK))
         load_x(0)
+        nc.scalar.dma_start(out=c16[:], in_=c.rearrange("(g p j) -> p g j", p=P, j=PACK))
         load_x(1)
         load_m(0)
         nc.scalar.dma_start(out=b_row[0:1, :], in_=b.rearrange("(o e) -> o e", o=1))
@@ -131,17 +139,17 @@ def tile_iv4rechubermomentmatrix_w4_kernel(tc, x, m_words, m_scales, b, y, c, z_
         load_z(1)
         load_x(2)
         load_x(3)
-        load_z(2)
         load_y(1)
+        load_z(2)
         load_x(4)
         load_x(5)
-        load_z(3)
-        load_y(2)
         load_x(6)
         load_x(7)
-        load_y(4)
+        load_y(2)
         load_y(3)
+        load_z(3)
         load_m(1)
+        load_y(4)
         load_y(5)
         load_m(2)
         load_y(6)
@@ -172,13 +180,18 @@ def tile_iv4rechubermomentmatrix_w4_kernel(tc, x, m_words, m_scales, b, y, c, z_
         def interleave(engine, grouped, planes):
             dst = grouped.rearrange("p (n i j) -> p n j i", i=4, j=PACK)
             src = planes.rearrange("p j (n i) -> p n j i", i=4)
-            if engine == "vector":
+            if engine == "gpsimd":
+                nc.gpsimd.tensor_scalar(
+                    out=grouped.rearrange("p (n j) -> p n j", j=PACK), in0=planes.rearrange("p j n -> p n j"),
+                    scalar1=1.0, scalar2=0.0, op0=ALU.mult, op1=ALU.add,
+                )
+            elif engine == "vector":
                 nc.vector.tensor_copy(out=dst, in_=src)
             else:
                 nc.scalar.copy(out=dst, in_=src)
 
         def turn_x(i):
-            x_turned[i] = bank(TURN_BANKS[i % 4])
+            x_turned[i] = side_bank()
             words = x_in[i][:].bitcast(F32)
             for kp in range(PASSES):
                 for u in range(2):
@@ -187,9 +200,9 @@ def tile_iv4rechubermomentmatrix_w4_kernel(tc, x, m_words, m_scales, b, y, c, z_
                         x_turned[i][:, col : col + P], words[:, 256 * kp + u : 256 * (kp + 1) : 2], ident32[:]
                     )
 
-        def copy_x(i):
+        def copy_x(i, engine="scalar"):
             x_grouped[i] = ring.tile([P, D], BF16, name="x_grouped", align_bytes=64)
-            nc.scalar.copy(
+            (nc.scalar.copy if engine == "scalar" else nc.vector.tensor_copy)(
                 out=x_grouped[i][:].bitcast(F32).rearrange("p (k r u) -> p k r u", k=PASSES, u=2),
                 in_=x_turned[i][:].rearrange("p (k u r) -> p k r u", k=PASSES, u=2),
             )
@@ -209,10 +222,10 @@ def tile_iv4rechubermomentmatrix_w4_kernel(tc, x, m_words, m_scales, b, y, c, z_
             else:
                 nc.scalar.activation(out=z_wide[i][:, j, :], in_=src, func=COPY, scale=zs[:, g, j : j + 1])
 
-        def group_z(i, engine, half):
+        def group_z(i, engine, lo=0, hi=8):
             if i not in z_grouped:
                 z_grouped[i] = kept("z_grouped%d" % i, [P, PACK * Z_COLS], BF16)
-            cols = slice(0, Z_COLS) if half is None else slice(half * Z_COLS // 2, (half + 1) * Z_COLS // 2)
+            cols = slice(lo * Z_COLS // 8, hi * Z_COLS // 8)
             interleave(engine, z_grouped[i][:, PACK * cols.start : PACK * cols.stop], z_wide[i][:, :, cols])
 
         def quantize_z(i):
@@ -224,64 +237,48 @@ def tile_iv4rechubermomentmatrix_w4_kernel(tc, x, m_words, m_scales, b, y, c, z_
             return y_in[s // 2][:, col : col + w]
 
         def spread_b():
-            spread = bank(TURN_BANKS[3])
-            nc.tensor.matmul(spread[:], lhsT=minus_ones[:], rhs=b_row[:, BANK:], start=True, stop=True)
-            w_bank["b"] = spread
-
-        def copy_b():
-            nc.scalar.copy(out=minus_b[:], in_=w_bank["b"][:])
-
-        def open_w(s):
-            ch, g, js = steps[s]
-            e0, w = CHUNKS[ch]
-            w_bank[s] = bank(W_BANKS[s % 2])
-            nc.tensor.matmul(w_bank[s][:], lhsT=minus_ones[:], rhs=b_row[:, e0 : e0 + w], start=True, stop=False)
-
-        def close_w(s):
-            nc.tensor.matmul(w_bank[s][:], lhsT=ident16[:], rhs=y_plane(s, 0), start=False, stop=True)
+            spread = side_bank()
+            nc.tensor.matmul(spread[:], lhsT=minus_ones[:], rhs=b_row[:, :BANK], start=True, stop=True)
+            nc.scalar.copy(out=minus_b[:], in_=spread[:])
 
         def y_minus_b(s):
             ch, g, js = steps[s]
             e0, w = CHUNKS[ch]
-            if on_vector(s):
-                return
-            w_bank[s] = bank(W_BANKS[s % 2] if s < wide_steps else W_BANKS[s // 2 % 2])
+            w_bank[s] = side_bank()
             for jj in range(len(js)):
                 dst = w_bank[s][:, jj * w : (jj + 1) * w]
                 nc.tensor.matmul(dst, lhsT=minus_ones[:], rhs=b_row[:, e0 : e0 + w], start=True, stop=False)
                 nc.tensor.matmul(dst, lhsT=ident16[:], rhs=y_plane(s, jj), start=False, stop=True)
 
-        def scale_w(s):
+        def scale_w(s, engine="scalar"):
             ch, g, js = steps[s]
             e0, w = CHUNKS[ch]
-            if on_vector(s):
-                cw[s] = kept("minus_cb%d" % s, [P, BANK], F32)
-            else:
-                cw[s] = ring.tile([P, BANK], F32, name="cw", align_bytes=64)
+            pool = ring if s in VS else deep
+            cw[s] = pool.tile([P, BANK], F32, name="minus_cb" if s in VS else "cw", align_bytes=64)
             for jj, j in enumerate(js):
                 cols = slice(jj * w, (jj + 1) * w)
-                src = minus_b[:, e0 - BANK : e0 - BANK + w] if on_vector(s) else w_bank[s][:, cols]
-                nc.scalar.activation(out=cw[s][:, cols], in_=src, func=COPY, scale=c32[:, g, j : j + 1])
+                src = minus_b[:] if s in VS else w_bank[s][:, cols]
+                if engine == "scalar":
+                    nc.scalar.activation(out=cw[s][:, cols], in_=src, func=COPY, scale=c32[:, g, j : j + 1])
+                else:
+                    nc.vector.tensor_scalar(
+                        out=cw[s][:, cols], in0=src, scalar1=c32[:, g, j : j + 1], scalar2=None, op0=ALU.mult
+                    )
 
         def add_cy(s):
             ch, g, js = steps[s]
-            e0, w = CHUNKS[ch]
-            if not on_vector(s):
-                return
             minus_cb = cw[s]
             cw[s] = ring.tile([P, BANK], F32, name="cw_sum", align_bytes=64)
-            for jj, j in enumerate(js):
-                cols = slice(jj * w, (jj + 1) * w)
-                nc.vector.scalar_tensor_tensor(
-                    out=cw[s][:, cols], in0=y_plane(s, jj), scalar=c32[:, g, j : j + 1], in1=minus_cb[:, cols],
-                    op0=ALU.mult, op1=ALU.add,
-                )
+            nc.vector.scalar_tensor_tensor(
+                out=cw[s][:], in0=y_plane(s, 0), scalar=c32[:, g, js[0] : js[0] + 1], in1=minus_cb[:],
+                op0=ALU.mult, op1=ALU.add,
+            )
 
         def first_product(s):
             ch, g, js = steps[s]
             e0, w = CHUNKS[ch]
             n = w if w == BANK else P
-            acc[s] = bank(ACC_BANKS[s % 2])
+            acc[s] = bank(ACC_BANKS[s % 4])
             for jj, j in enumerate(js):
                 codes, scales = x_q[g * PACK + j]
                 for n0 in range(0, w, n):
@@ -307,41 +304,49 @@ def tile_iv4rechubermomentmatrix_w4_kernel(tc, x, m_words, m_scales, b, y, c, z_
                     op0=ALU.mult, op1=ALU.subtract,
                 )
 
-        def clip(s, only=None):
+        def clip(s):
             ch, g, js = steps[s]
-            e0, w = CHUNKS[ch]
-            if (ch, g) not in t_planes:
-                t_planes[ch, g] = kept("t_planes%d_%d" % (ch, g), [P, PACK, w], BF16)
+            w = CHUNKS[ch][1]
+            batch = s // PACK
+            if batch not in t_planes:
+                t_planes[batch] = kept("t_planes%d" % batch, [P, PACK, BANK], BF16)
+            col = g * w % BANK
             for jj, j in enumerate(js):
-                if (only is not None and jj != only) or (only is None and s == 8 and jj == 0):
-                    continue
                 nc.vector.tensor_scalar(
-                    out=t_planes[ch, g][:, j, :], in0=pre[s][:, jj * w : (jj + 1) * w],
+                    out=t_planes[batch][:, j, col : col + w], in0=pre[s][:, jj * w : (jj + 1) * w],
                     scalar1=c_hi[:, g, j : j + 1], scalar2=c_lo[:, g, j : j + 1], op0=ALU.min, op1=ALU.max,
                 )
 
-        def closes_group(s):
-            return steps[s][2][-1] == PACK - 1
+        def group_t(batch, engine, lo, hi):
+            if batch not in t_grouped:
+                t_grouped[batch] = kept("t_grouped%d" % batch, [P, PACK * BANK], BF16)
+            interleave(engine, t_grouped[batch][:, PACK * lo : PACK * hi], t_planes[batch][:, :, lo:hi])
 
-        def group_t(s, engine):
-            ch, g, js = steps[s]
-            t_grouped[ch, g] = kept("t_grouped%d_%d" % (ch, g), [P, PACK * CHUNKS[ch][1]], BF16)
-            interleave(engine, t_grouped[ch, g][:], t_planes[ch, g][:])
-
-        def quantize_t(s):
-            ch, g, js = steps[s]
-            t_q[ch, g] = quantize("t%d_%d" % (ch, g), t_grouped[ch, g], CHUNKS[ch][1])
+        def quantize_t(batch, lo, hi):
+            if batch not in t_q:
+                t_q[batch] = (
+                    kept("t_codes%d" % batch, [P, BANK], U32),
+                    kept("t_scales%d" % batch, [P, BANK], U8),
+                )
+            codes, scales = t_q[batch]
+            nc.vector.quantize_mx(
+                out=codes[:, lo:hi].bitcast(FP8X4),
+                scales=scales[:, lo:hi],
+                in_=t_grouped[batch][:, PACK * lo : PACK * hi],
+            )
 
         def second_pass(ch, k, g, dst):
+            w = CHUNKS[ch][1]
             z_codes, z_scales = z_q[g, k * P // Z_COLS]
-            t_codes, t_scales = t_q[ch, g]
+            t_codes, t_scales = t_q[g if ch == 0 else ch + 1]
             q0 = k * P % Z_COLS
+            col = g * w % BANK
             nc.tensor.matmul_mx(
                 out=dst,
                 lhsT=z_codes[:, q0 : q0 + P].bitcast(FP8X4),
                 lhsT_scale=z_scales[:, q0 : q0 + P],
-                rhs=t_codes[:].bitcast(FP8X4),
-                rhs_scale=t_scales[:],
+                rhs=t_codes[:, col : col + w].bitcast(FP8X4),
+                rhs_scale=t_scales[:, col : col + w],
                 start=(g == 0),
                 stop=(g == PASSES - 1),
             )
@@ -349,17 +354,10 @@ def tile_iv4rechubermomentmatrix_w4_kernel(tc, x, m_words, m_scales, b, y, c, z_
         def second_product(ch, i):
             w = CHUNKS[ch][1]
             per_bank = BANK // w
-            out_bank[ch, i] = bank(TURN_BANKS[i % 4])
+            out_bank[ch, i] = side_bank()
             for kk in range(per_bank):
                 for g in range(PASSES):
                     second_pass(ch, i * per_bank + kk, g, out_bank[ch, i][:, kk * w : (kk + 1) * w])
-
-        def open_out(i):
-            out_bank[0, i] = bank(TURN_BANKS[i])
-            second_pass(0, i, 0, out_bank[0, i][:])
-
-        def close_out(i):
-            second_pass(0, i, 1, out_bank[0, i][:])
 
         def store(ch, src, k0, blocks, engine):
             e0, w = CHUNKS[ch]
@@ -372,9 +370,9 @@ def tile_iv4rechubermomentmatrix_w4_kernel(tc, x, m_words, m_scales, b, y, c, z_
                 out=out_rows[:, k0 : k0 + blocks, e0 : e0 + w], in_=result[:].rearrange("p (k e) -> p k e", k=blocks)
             )
 
-        def store_bank(ch, i):
+        def store_bank(ch, i, engine="scalar"):
             per_bank = BANK // CHUNKS[ch][1]
-            store(ch, out_bank[ch, i][:], i * per_bank, per_bank, "scalar")
+            store(ch, out_bank[ch, i][:], i * per_bank, per_bank, engine)
 
         for j in range(3):
             widen_z(0, j, "vector")
@@ -383,110 +381,111 @@ def tile_iv4rechubermomentmatrix_w4_kernel(tc, x, m_words, m_scales, b, y, c, z_
         nc.vector.scalar_tensor_tensor(out=c_hi[:], in0=c16[:], scalar=-1.0, in1=c16[:], op0=ALU.mult, op1=ALU.max)
         nc.vector.scalar_tensor_tensor(out=c_lo[:], in0=c16[:], scalar=-1.0, in1=c16[:], op0=ALU.mult, op1=ALU.min)
         turn_x(0)
-        spread_b()
-        open_w(0)
         copy_x(0)
-        copy_b()
         turn_x(1)
         copy_x(1)
-        open_w(1)
-        group_z(0, "vector", None)
+        spread_b()
+        group_z(0, "vector")
         quantize_x(0)
         quantize_z(0)
         quantize_x(1)
-        scale_w(9)
-        scale_w(11)
-        scale_w(13)
-        close_w(0)
-        scale_w(0)
-        scale_w(15)
-        for j in range(PACK):
+        for s in range(3):
+            scale_w(s)
+        first_product(0)
+        turn_x(2)
+        copy_x(2)
+        turn_x(3)
+        copy_x(3)
+        first_product(1)
+        scale_w(3)
+        add_cy(0)
+        add_cy(1)
+        for j in range(PACK - 1):
             widen_z(1, j, "vector")
-
-        widen_jobs = [(i, j) for i in range(2, len(z_pieces)) for j in range(PACK)]
-        for s in range(n_steps + 1):
-            if 1 <= s < wide_steps:
-                y_minus_b(s + 1)
-            elif s >= wide_steps and s + 2 < n_steps:
-                y_minus_b(s + 2)
-            if s < n_steps:
-                first_product(s)
-            if s == 0:
-                close_w(1)
-            if s in (0, 1, 3):
-                turn_x(s + 2 + s % 2)
-                turn_x(s + 3 + s % 2)
-            if s in (6, 7):
-                open_out(2 * (s - 6))
-                open_out(2 * (s - 6) + 1)
-            if s == 10:
-                for i in range(4):
-                    close_out(i)
-            if s in (11, 12):
-                second_product(0, 2 * s - 18)
-                second_product(0, 2 * s - 17)
-            if s in (14, 15):
-                second_product(1, 2 * s - 28)
-                second_product(1, 2 * s - 27)
-            if s < wide_steps:
-                scale_w(s + 1)
-            elif s + 2 < n_steps and not on_vector(s + 2):
-                scale_w(s + 2)
-            if s < 2:
-                copy_x(2 * s + 2)
-                copy_x(2 * s + 3)
-            if s in (3, 4):
-                copy_x(s + 3)
-            for i, j in widen_jobs[WJ[min(s, 7)] : WJ[min(s + 1, 7)]]:
-                widen_z(i, j, "scalar")
-            if s in (3, 4):
-                group_z(2, "scalar", s - 3)
-            if s == 7:
-                group_z(3, "scalar", 0)
-                group_z(3, "scalar", 1)
-            if s == 10:
-                for i in range(3):
-                    store_bank(0, i)
-            if s in CY:
-                add_cy(9 + 2 * CY.index(s))
-            if s == 1:
-                quantize_x(2)
-            if 2 <= s and s + 2 < n_slots:
-                quantize_x(s + 2)
-            if s >= 1:
-                clip(s - 1)
-            if s < n_steps:
-                residual(s)
-            if s == 1:
-                quantize_x(3)
-            if s in ZQ:
-                quantize_z(ZQ.index(s) + 1)
-            if s == 0:
-                group_z(1, "vector", None)
-            if s >= 1 and closes_group(s - 1):
-                group_t(s - 1, "scalar" if s in TS else "vector")
-            if s >= 2 and closes_group(s - 2) and s != 9:
-                quantize_t(s - 2)
-            if s == 8:
-                clip(8, 0)
-                quantize_t(7)
-            if s == 10:
-                store_bank(0, 3)
-            if s in (11, 12):
-                store_bank(0, 2 * s - 18)
-                store_bank(0, 2 * s - 17)
-            if s in (14, 15):
-                store_bank(1, 2 * s - 28)
-                store_bank(1, 2 * s - 27)
-            if s == n_steps:
-                last = len(CHUNKS) - 1
-                w = CHUNKS[last][1]
-                order = W_BANKS + TURN_BANKS + ACC_BANKS
-                for k in range(Q // P):
-                    out_bank[last, k] = bank(order[k])
-                    second_pass(last, k, 0, out_bank[last, k][:, :w])
-
-        quantize_t(n_steps - 1)
+        quantize_x(2)
+        add_cy(2)
+        quantize_x(3)
+        add_cy(3)
+        first_product(2)
+        first_product(3)
+        for j in range(PACK):
+            widen_z(2, j, "scalar")
+        for i in range(4, 8):
+            turn_x(i)
+        for i in range(4, 8):
+            copy_x(i)
+        widen_z(1, PACK - 1, "vector")
+        group_z(1, "gpsimd", 0, GS)
+        for s in range(4):
+            residual(s)
+        group_z(1, "vector", GS, 8)
+        for s in range(4, 8):
+            y_minus_b(s)
+            scale_w(s)
+        for s in range(4, 7):
+            quantize_x(s)
+        quantize_z(1)
+        quantize_x(7)
+        for s in range(4, 8):
+            first_product(s)
+        for s in range(4):
+            clip(s)
+        group_t(0, "gpsimd", 0, GS * 64)
+        for s in range(4, 8):
+            residual(s)
+        group_t(0, "vector", GS * 64, BANK)
+        group_z(2, "scalar")
+        for j in range(PACK):
+            widen_z(3, j, "scalar")
+        for s in range(8, 12):
+            y_minus_b(s)
+            scale_w(s)
+        for s in range(8, 12):
+            first_product(s)
+        quantize_z(2)
+        quantize_t(0, 0, BANK)
+        for s in range(4, 8):
+            clip(s)
+        group_t(1, "gpsimd", 0, GS * 64)
+        for s in range(8, 12):
+            residual(s)
+        group_t(1, "vector", GS * 64, BANK)
+        group_z(3, "scalar")
+        for s in range(12, 16):
+            y_minus_b(s)
+            scale_w(s)
+        for s in range(12, 16):
+            first_product(s)
+        clip(8)
+        quantize_t(1, 0, BANK)
+        clip(9)
+        clip(10)
+        quantize_z(3)
+        clip(11)
+        group_t(2, "gpsimd", 0, GS * 64)
+        for s in range(12, 16):
+            residual(s)
+        group_t(2, "vector", GS * 64, BANK)
+        for i in range(8):
+            second_product(0, i)
+            store_bank(0, i)
+        clip(12)
+        quantize_t(2, 0, BANK)
+        clip(13)
+        clip(14)
+        group_t(3, "vector", 0, BANK // 2)
+        clip(15)
+        quantize_t(3, 0, BANK // 2)
+        group_t(3, "vector", BANK // 2, BANK)
+        for i in range(4):
+            second_product(1, i)
+            store_bank(1, i)
+        last = len(CHUNKS) - 1
+        w = CHUNKS[last][1]
+        for k in range(Q // P):
+            out_bank[last, k] = bank(ACC_BANKS[k]) if k < len(ACC_BANKS) else side_bank()
+            second_pass(last, k, 0, out_bank[last, k][:, :w])
+        quantize_t(3, BANK // 2, BANK)
         for k in range(Q // P):
             second_pass(last, k, 1, out_bank[last, k][:, :w])
-            store(last, out_bank[last, k][:, :w], k, 1, "scalar" if k % 2 == 0 else "vector")
+            store(last, out_bank[last, k][:, :w], k, 1, "scalar" if k % 2 == 1 else "vector")

@@ -22,22 +22,16 @@ P = 128
 PACK = 4
 PASSES = 2
 BANK = 512
+BATCH = 4
 CHUNKS = ((0, 512), (512, 256), (768, 256))
 Z_COLS = 512
+RUN = 4
+GPSIMD_COLS = 384
+SCALAR_COLS = 384
 OUT_SCALE = 1.0 / math.sqrt(B)
 
 ACC_BANKS = (2, 3, 6, 7)
 SIDE_BANKS = (0, 1, 4, 5)
-TS = ()
-VS = (0, 1, 2, 3)
-GS = 6
-ZV = 3
-REST = "vector"
-Z1V = 4
-ZG = {(1, None): (0, "vector"), (2, 0): (3, "scalar"), (2, 1): (4, "scalar"), (3, 0): (7, "scalar"), (3, 1): (7, "scalar")}
-ZQ = (1, 6, 9)
-WJ = (0, 1, 2, 4, 4, 4, 7, 8)
-OJ = (0, 2, 4, 6, 8, 8, 10, 12)
 
 
 def tile_iv4rechubermomentmatrix_w4_kernel(tc, x, m_words, m_scales, b, y, c, z_bytes, z_scale, out):
@@ -49,10 +43,7 @@ def tile_iv4rechubermomentmatrix_w4_kernel(tc, x, m_words, m_scales, b, y, c, z_
         for g in range(PASSES):
             for j0 in range(0, PACK, per_bank):
                 steps.append((ch, g, range(j0, j0 + per_bank)))
-    n_steps = len(steps)
-    n_slots = PASSES * PACK
-    wide_steps = PASSES * PACK
-    z_pieces = [(g, h) for h in range(Q // Z_COLS) for g in range(PASSES)]
+    z_pieces = [(g, h) for g in range(PASSES) for h in range(Q // Z_COLS)]
 
     x_rows = x.rearrange("(g p j) d -> g j p d", p=P, j=PACK)
     y_rows = y.rearrange("(g p j) e -> g p j e", p=P, j=PACK)
@@ -61,22 +52,22 @@ def tile_iv4rechubermomentmatrix_w4_kernel(tc, x, m_words, m_scales, b, y, c, z_
 
     with ExitStack() as ctx:
         keep = ctx.enter_context(tc.tile_pool(name="keep", bufs=1))
-        ring = ctx.enter_context(tc.tile_pool(name="ring", bufs=4))
-        deep = ctx.enter_context(tc.tile_pool(name="deep", bufs=8))
+        ring = ctx.enter_context(tc.tile_pool(name="ring", bufs=BATCH))
+        deep = ctx.enter_context(tc.tile_pool(name="deep", bufs=2 * BATCH))
         psum = ctx.enter_context(tc.psum_pool(name="psum", bufs=1))
         ctx.enter_context(tc.manual_schedule())
-
-        side_uses = []
-
-        def side_bank():
-            side_uses.append(None)
-            return bank(SIDE_BANKS[(len(side_uses) - 1) % len(SIDE_BANKS)])
 
         def kept(name, shape, dtype):
             return keep.tile(shape, dtype, name=name, align_bytes=64)
 
         def bank(index):
             return psum.tile([P, BANK], F32, name="bank%d" % index)
+
+        side_taken = []
+
+        def side_bank():
+            side_taken.append(SIDE_BANKS[len(side_taken) % len(SIDE_BANKS)])
+            return bank(side_taken[-1])
 
         m_scale = kept("m_scale", [P, PASSES, E], U8)
         b_row = kept("b_row", [P, E], BF16)
@@ -90,9 +81,9 @@ def tile_iv4rechubermomentmatrix_w4_kernel(tc, x, m_words, m_scales, b, y, c, z_
         c_lo = kept("c_lo", [P, PASSES, PACK], F32)
         minus_b = kept("minus_b", [P, BANK], F32)
 
-        x_in = [kept("x_in%d" % i, [P, D], BF16) for i in range(n_slots)]
-        y_in = [kept("y_in%d" % i, [P, 2 * BANK], BF16) for i in range(n_steps // 2)]
-        z_in = [kept("z_in%d" % i, [P, PACK, Z_COLS], U8) for i in range(len(z_pieces))]
+        x_in = [kept("x_in%d" % i, [P, D], BF16) for i in range(PASSES * PACK)]
+        y_in = [kept("y_in%d" % i, [P, 2 * BANK], BF16) for i in range(len(steps) // 2)]
+        z_in = [kept("z_in%d" % i, [P, 2, Q], U8) for i in range(2 * PASSES)]
         m_in = [kept("m_in%d" % ch, [P, PASSES, 2 * w], U8) for ch, (e0, w) in enumerate(CHUNKS)]
 
         def load_x(i):
@@ -108,8 +99,7 @@ def tile_iv4rechubermomentmatrix_w4_kernel(tc, x, m_words, m_scales, b, y, c, z_
             )
 
         def load_z(i):
-            g, h = z_pieces[i]
-            nc.sync.dma_start(out=z_in[i][:], in_=z_rows[g][:, :, h * Z_COLS : (h + 1) * Z_COLS])
+            nc.sync.dma_start(out=z_in[i][:], in_=z_rows[i // 2][:, 2 * (i % 2) : 2 * (i % 2) + 2, :])
 
         def load_m(ch):
             e0, w = CHUNKS[ch]
@@ -127,49 +117,35 @@ def tile_iv4rechubermomentmatrix_w4_kernel(tc, x, m_words, m_scales, b, y, c, z_
         nc.scalar.dma_start(out=zs[:], in_=z_scale.rearrange("(g p j) o -> p g (j o)", p=P, j=PACK))
         load_x(0)
         nc.scalar.dma_start(out=c16[:], in_=c.rearrange("(g p j) -> p g j", p=P, j=PACK))
+        load_z(1)
         load_x(1)
-        load_m(0)
         nc.scalar.dma_start(out=b_row[0:1, :], in_=b.rearrange("(o e) -> o e", o=1))
         for quad in range(4):
             nc.sync.dma_start(
                 out=m_scale[32 * quad : 32 * quad + 4].bitcast(I32),
                 in_=m_scales[:, 4 * quad : 4 * quad + 4, :].rearrange("g r n -> r g n").bitcast(I32),
             )
+        load_m(0)
         load_y(0)
-        load_z(1)
         load_x(2)
         load_x(3)
         load_y(1)
         load_z(2)
-        load_x(4)
-        load_x(5)
-        load_x(6)
-        load_x(7)
+        for i in range(PACK, 2 * PACK):
+            load_x(i)
         load_y(2)
         load_y(3)
         load_z(3)
-        load_m(1)
-        load_y(4)
-        load_y(5)
-        load_m(2)
-        load_y(6)
-        load_y(7)
+        for ch in (1, 2):
+            load_m(ch)
+            load_y(2 + 2 * ch)
+            load_y(3 + 2 * ch)
         nc.scalar.copy(out=ident16[:], in_=ident32[:])
 
-        x_turned = {}
-        x_grouped = {}
-        x_q = {}
-        z_wide = {}
-        z_grouped = {}
-        z_q = {}
-        w_bank = {}
-        cw = {}
-        acc = {}
-        pre = {}
-        t_planes = {}
-        t_grouped = {}
-        t_q = {}
-        out_bank = {}
+        x_turned, x_grouped, x_q = {}, {}, {}
+        z_wide, z_grouped, z_q = {}, {}, {}
+        w_bank, minus_cb, cw, acc, unclipped = {}, {}, {}, {}, {}
+        t_planes, t_grouped, t_q = {}, {}, {}
 
         def quantize(name, grouped, cols):
             codes = kept(name + "_codes", [P, cols], U32)
@@ -178,14 +154,19 @@ def tile_iv4rechubermomentmatrix_w4_kernel(tc, x, m_words, m_scales, b, y, c, z_
             return codes, scales
 
         def interleave(engine, grouped, planes):
-            dst = grouped.rearrange("p (n i j) -> p n j i", i=4, j=PACK)
-            src = planes.rearrange("p j (n i) -> p n j i", i=4)
             if engine == "gpsimd":
                 nc.gpsimd.tensor_scalar(
-                    out=grouped.rearrange("p (n j) -> p n j", j=PACK), in0=planes.rearrange("p j n -> p n j"),
-                    scalar1=1.0, scalar2=0.0, op0=ALU.mult, op1=ALU.add,
+                    out=grouped.rearrange("p (n j) -> p n j", j=PACK),
+                    in0=planes.rearrange("p j n -> p n j"),
+                    scalar1=1.0,
+                    scalar2=0.0,
+                    op0=ALU.mult,
+                    op1=ALU.add,
                 )
-            elif engine == "vector":
+                return
+            dst = grouped.rearrange("p (n i j) -> p n j i", i=RUN, j=PACK)
+            src = planes.rearrange("p j (n i) -> p n j i", i=RUN)
+            if engine == "vector":
                 nc.vector.tensor_copy(out=dst, in_=src)
             else:
                 nc.scalar.copy(out=dst, in_=src)
@@ -197,12 +178,12 @@ def tile_iv4rechubermomentmatrix_w4_kernel(tc, x, m_words, m_scales, b, y, c, z_
                 for u in range(2):
                     col = (2 * kp + u) * P
                     nc.tensor.transpose(
-                        x_turned[i][:, col : col + P], words[:, 256 * kp + u : 256 * (kp + 1) : 2], ident32[:]
+                        x_turned[i][:, col : col + P], words[:, 2 * P * kp + u : 2 * P * (kp + 1) : 2], ident32[:]
                     )
 
-        def copy_x(i, engine="scalar"):
+        def copy_x(i):
             x_grouped[i] = ring.tile([P, D], BF16, name="x_grouped", align_bytes=64)
-            (nc.scalar.copy if engine == "scalar" else nc.vector.tensor_copy)(
+            nc.scalar.copy(
                 out=x_grouped[i][:].bitcast(F32).rearrange("p (k r u) -> p k r u", k=PASSES, u=2),
                 in_=x_turned[i][:].rearrange("p (k u r) -> p k r u", k=PASSES, u=2),
             )
@@ -210,23 +191,22 @@ def tile_iv4rechubermomentmatrix_w4_kernel(tc, x, m_words, m_scales, b, y, c, z_
         def quantize_x(i):
             x_q[i] = quantize("x%d" % i, x_grouped[i], PASSES * P)
 
-        def widen_z(i, j, engine):
-            g, h = z_pieces[i]
-            if i not in z_wide:
-                z_wide[i] = kept("z_wide%d" % i, [P, PACK, Z_COLS], BF16)
-            src = z_in[i][:, j, :].bitcast(FP8)
+        def widen_z(g, j, engine, lo=0, hi=Q):
+            if g not in z_wide:
+                z_wide[g] = kept("z_wide%d" % g, [P, PACK, Q], BF16)
+            src = z_in[2 * g + j // 2][:, j % 2, lo:hi].bitcast(FP8)
+            dst = z_wide[g][:, j, lo:hi]
             if engine == "vector":
-                nc.vector.tensor_scalar(
-                    out=z_wide[i][:, j, :], in0=src, scalar1=zs[:, g, j : j + 1], scalar2=None, op0=ALU.mult
-                )
+                nc.vector.tensor_scalar(out=dst, in0=src, scalar1=zs[:, g, j : j + 1], scalar2=None, op0=ALU.mult)
             else:
-                nc.scalar.activation(out=z_wide[i][:, j, :], in_=src, func=COPY, scale=zs[:, g, j : j + 1])
+                nc.scalar.activation(out=dst, in_=src, func=COPY, scale=zs[:, g, j : j + 1])
 
-        def group_z(i, engine, lo=0, hi=8):
+        def group_z(i, engine, lo=0, hi=Z_COLS):
+            g, h = z_pieces[i]
             if i not in z_grouped:
                 z_grouped[i] = kept("z_grouped%d" % i, [P, PACK * Z_COLS], BF16)
-            cols = slice(lo * Z_COLS // 8, hi * Z_COLS // 8)
-            interleave(engine, z_grouped[i][:, PACK * cols.start : PACK * cols.stop], z_wide[i][:, :, cols])
+            q0 = h * Z_COLS
+            interleave(engine, z_grouped[i][:, PACK * lo : PACK * hi], z_wide[g][:, :, q0 + lo : q0 + hi])
 
         def quantize_z(i):
             z_q[z_pieces[i]] = quantize("z%d" % i, z_grouped[i], Z_COLS)
@@ -241,7 +221,24 @@ def tile_iv4rechubermomentmatrix_w4_kernel(tc, x, m_words, m_scales, b, y, c, z_
             nc.tensor.matmul(spread[:], lhsT=minus_ones[:], rhs=b_row[:, :BANK], start=True, stop=True)
             nc.scalar.copy(out=minus_b[:], in_=spread[:])
 
-        def y_minus_b(s):
+        def scale_b(s):
+            ch, g, js = steps[s]
+            minus_cb[s] = ring.tile([P, BANK], F32, name="minus_cb", align_bytes=64)
+            nc.scalar.activation(out=minus_cb[s][:], in_=minus_b[:], func=COPY, scale=c32[:, g, js[0] : js[0] + 1])
+
+        def add_cy(s):
+            ch, g, js = steps[s]
+            cw[s] = ring.tile([P, BANK], F32, name="cw_first", align_bytes=64)
+            nc.vector.scalar_tensor_tensor(
+                out=cw[s][:],
+                in0=y_plane(s, 0),
+                scalar=c32[:, g, js[0] : js[0] + 1],
+                in1=minus_cb[s][:],
+                op0=ALU.mult,
+                op1=ALU.add,
+            )
+
+        def make_cw(s):
             ch, g, js = steps[s]
             e0, w = CHUNKS[ch]
             w_bank[s] = side_bank()
@@ -249,36 +246,16 @@ def tile_iv4rechubermomentmatrix_w4_kernel(tc, x, m_words, m_scales, b, y, c, z_
                 dst = w_bank[s][:, jj * w : (jj + 1) * w]
                 nc.tensor.matmul(dst, lhsT=minus_ones[:], rhs=b_row[:, e0 : e0 + w], start=True, stop=False)
                 nc.tensor.matmul(dst, lhsT=ident16[:], rhs=y_plane(s, jj), start=False, stop=True)
-
-        def scale_w(s, engine="scalar"):
-            ch, g, js = steps[s]
-            e0, w = CHUNKS[ch]
-            pool = ring if s in VS else deep
-            cw[s] = pool.tile([P, BANK], F32, name="minus_cb" if s in VS else "cw", align_bytes=64)
+            cw[s] = deep.tile([P, BANK], F32, name="cw", align_bytes=64)
             for jj, j in enumerate(js):
                 cols = slice(jj * w, (jj + 1) * w)
-                src = minus_b[:] if s in VS else w_bank[s][:, cols]
-                if engine == "scalar":
-                    nc.scalar.activation(out=cw[s][:, cols], in_=src, func=COPY, scale=c32[:, g, j : j + 1])
-                else:
-                    nc.vector.tensor_scalar(
-                        out=cw[s][:, cols], in0=src, scalar1=c32[:, g, j : j + 1], scalar2=None, op0=ALU.mult
-                    )
-
-        def add_cy(s):
-            ch, g, js = steps[s]
-            minus_cb = cw[s]
-            cw[s] = ring.tile([P, BANK], F32, name="cw_sum", align_bytes=64)
-            nc.vector.scalar_tensor_tensor(
-                out=cw[s][:], in0=y_plane(s, 0), scalar=c32[:, g, js[0] : js[0] + 1], in1=minus_cb[:],
-                op0=ALU.mult, op1=ALU.add,
-            )
+                nc.scalar.activation(out=cw[s][:, cols], in_=w_bank[s][:, cols], func=COPY, scale=c32[:, g, j : j + 1])
 
         def first_product(s):
             ch, g, js = steps[s]
             e0, w = CHUNKS[ch]
             n = w if w == BANK else P
-            acc[s] = bank(ACC_BANKS[s % 4])
+            acc[s] = bank(ACC_BANKS[s % BATCH])
             for jj, j in enumerate(js):
                 codes, scales = x_q[g * PACK + j]
                 for n0 in range(0, w, n):
@@ -293,28 +270,37 @@ def tile_iv4rechubermomentmatrix_w4_kernel(tc, x, m_words, m_scales, b, y, c, z_
                             stop=(kp == PASSES - 1),
                         )
 
-        def residual(s):
-            ch, g, js = steps[s]
-            e0, w = CHUNKS[ch]
-            pre[s] = ring.tile([P, BANK], F32, name="pre", align_bytes=64)
-            for jj, j in enumerate(js):
-                cols = slice(jj * w, (jj + 1) * w)
-                nc.vector.scalar_tensor_tensor(
-                    out=pre[s][:, cols], in0=acc[s][:, cols], scalar=c32[:, g, j : j + 1], in1=cw[s][:, cols],
-                    op0=ALU.mult, op1=ALU.subtract,
-                )
+        def residuals(batch):
+            for s in range(BATCH * batch, BATCH * (batch + 1)):
+                ch, g, js = steps[s]
+                w = CHUNKS[ch][1]
+                unclipped[s] = ring.tile([P, BANK], F32, name="unclipped", align_bytes=64)
+                for jj, j in enumerate(js):
+                    cols = slice(jj * w, (jj + 1) * w)
+                    nc.vector.scalar_tensor_tensor(
+                        out=unclipped[s][:, cols],
+                        in0=acc[s][:, cols],
+                        scalar=c32[:, g, j : j + 1],
+                        in1=cw[s][:, cols],
+                        op0=ALU.mult,
+                        op1=ALU.subtract,
+                    )
 
         def clip(s):
             ch, g, js = steps[s]
             w = CHUNKS[ch][1]
-            batch = s // PACK
+            batch = s // BATCH
             if batch not in t_planes:
                 t_planes[batch] = kept("t_planes%d" % batch, [P, PACK, BANK], BF16)
             col = g * w % BANK
             for jj, j in enumerate(js):
                 nc.vector.tensor_scalar(
-                    out=t_planes[batch][:, j, col : col + w], in0=pre[s][:, jj * w : (jj + 1) * w],
-                    scalar1=c_hi[:, g, j : j + 1], scalar2=c_lo[:, g, j : j + 1], op0=ALU.min, op1=ALU.max,
+                    out=t_planes[batch][:, j, col : col + w],
+                    in0=unclipped[s][:, jj * w : (jj + 1) * w],
+                    scalar1=c_hi[:, g, j : j + 1],
+                    scalar2=c_lo[:, g, j : j + 1],
+                    op0=ALU.min,
+                    op1=ALU.max,
                 )
 
         def group_t(batch, engine, lo, hi):
@@ -322,12 +308,9 @@ def tile_iv4rechubermomentmatrix_w4_kernel(tc, x, m_words, m_scales, b, y, c, z_
                 t_grouped[batch] = kept("t_grouped%d" % batch, [P, PACK * BANK], BF16)
             interleave(engine, t_grouped[batch][:, PACK * lo : PACK * hi], t_planes[batch][:, :, lo:hi])
 
-        def quantize_t(batch, lo, hi):
+        def quantize_t(batch, lo=0, hi=BANK):
             if batch not in t_q:
-                t_q[batch] = (
-                    kept("t_codes%d" % batch, [P, BANK], U32),
-                    kept("t_scales%d" % batch, [P, BANK], U8),
-                )
+                t_q[batch] = (kept("t_codes%d" % batch, [P, BANK], U32), kept("t_scales%d" % batch, [P, BANK], U8))
             codes, scales = t_q[batch]
             nc.vector.quantize_mx(
                 out=codes[:, lo:hi].bitcast(FP8X4),
@@ -335,157 +318,138 @@ def tile_iv4rechubermomentmatrix_w4_kernel(tc, x, m_words, m_scales, b, y, c, z_
                 in_=t_grouped[batch][:, PACK * lo : PACK * hi],
             )
 
-        def second_pass(ch, k, g, dst):
-            w = CHUNKS[ch][1]
-            z_codes, z_scales = z_q[g, k * P // Z_COLS]
-            t_codes, t_scales = t_q[g if ch == 0 else ch + 1]
-            q0 = k * P % Z_COLS
-            col = g * w % BANK
-            nc.tensor.matmul_mx(
-                out=dst,
-                lhsT=z_codes[:, q0 : q0 + P].bitcast(FP8X4),
-                lhsT_scale=z_scales[:, q0 : q0 + P],
-                rhs=t_codes[:, col : col + w].bitcast(FP8X4),
-                rhs_scale=t_scales[:, col : col + w],
-                start=(g == 0),
-                stop=(g == PASSES - 1),
-            )
-
-        def second_product(ch, i):
-            w = CHUNKS[ch][1]
-            per_bank = BANK // w
-            out_bank[ch, i] = side_bank()
-            for kk in range(per_bank):
-                for g in range(PASSES):
-                    second_pass(ch, i * per_bank + kk, g, out_bank[ch, i][:, kk * w : (kk + 1) * w])
-
-        def store(ch, src, k0, blocks, engine):
+        def second_product(ch, k0, blocks, dst, engine):
             e0, w = CHUNKS[ch]
-            result = keep.tile([P, blocks * w], F32, name="result%d_%d" % (ch, k0), align_bytes=64)
+            for kk in range(blocks):
+                q0 = (k0 + kk) * P
+                for g in range(PASSES):
+                    z_codes, z_scales = z_q[g, q0 // Z_COLS]
+                    t_codes, t_scales = t_q[g if ch == 0 else ch + 1]
+                    z_cols = slice(q0 % Z_COLS, q0 % Z_COLS + P)
+                    t_cols = slice(g * w % BANK, g * w % BANK + w)
+                    nc.tensor.matmul_mx(
+                        out=dst[:, kk * w : (kk + 1) * w],
+                        lhsT=z_codes[:, z_cols].bitcast(FP8X4),
+                        lhsT_scale=z_scales[:, z_cols],
+                        rhs=t_codes[:, t_cols].bitcast(FP8X4),
+                        rhs_scale=t_scales[:, t_cols],
+                        start=(g == 0),
+                        stop=(g == PASSES - 1),
+                    )
+            result = kept("result%d_%d" % (ch, k0), [P, blocks * w], F32)
             if engine == "vector":
-                nc.vector.tensor_scalar(out=result[:], in0=src, scalar1=OUT_SCALE, scalar2=None, op0=ALU.mult)
+                nc.vector.tensor_scalar(
+                    out=result[:], in0=dst[:, : blocks * w], scalar1=OUT_SCALE, scalar2=None, op0=ALU.mult
+                )
             else:
-                nc.scalar.activation(out=result[:], in_=src, func=COPY, scale=OUT_SCALE)
+                nc.scalar.activation(out=result[:], in_=dst[:, : blocks * w], func=COPY, scale=OUT_SCALE)
             nc.sync.dma_start(
                 out=out_rows[:, k0 : k0 + blocks, e0 : e0 + w], in_=result[:].rearrange("p (k e) -> p k e", k=blocks)
             )
 
-        def store_bank(ch, i, engine="scalar"):
-            per_bank = BANK // CHUNKS[ch][1]
-            store(ch, out_bank[ch, i][:], i * per_bank, per_bank, engine)
 
-        for j in range(3):
-            widen_z(0, j, "vector")
-        widen_z(0, 3, "scalar")
+        widen_z(0, 0, "vector")
+        widen_z(0, 1, "scalar")
+        spread_b()
         nc.vector.tensor_copy(out=c32[:], in_=c16[:])
         nc.vector.scalar_tensor_tensor(out=c_hi[:], in0=c16[:], scalar=-1.0, in1=c16[:], op0=ALU.mult, op1=ALU.max)
         nc.vector.scalar_tensor_tensor(out=c_lo[:], in0=c16[:], scalar=-1.0, in1=c16[:], op0=ALU.mult, op1=ALU.min)
-        turn_x(0)
-        copy_x(0)
-        turn_x(1)
-        copy_x(1)
-        spread_b()
-        group_z(0, "vector")
+        for i in (0, 1):
+            turn_x(i)
+            copy_x(i)
+        widen_z(0, 2, "vector")
+        widen_z(0, 3, "vector", 0, Z_COLS)
         quantize_x(0)
-        quantize_z(0)
+        group_z(0, "vector")
         quantize_x(1)
-        for s in range(3):
-            scale_w(s)
+        quantize_z(0)
+        for s in (0, 1, 2):
+            scale_b(s)
         first_product(0)
-        turn_x(2)
-        copy_x(2)
-        turn_x(3)
-        copy_x(3)
+        for i in (2, 3):
+            turn_x(i)
+            copy_x(i)
         first_product(1)
-        scale_w(3)
+        scale_b(3)
         add_cy(0)
         add_cy(1)
-        for j in range(PACK - 1):
-            widen_z(1, j, "vector")
-        quantize_x(2)
-        add_cy(2)
-        quantize_x(3)
-        add_cy(3)
+        for s in (2, 3):
+            quantize_x(s)
+            add_cy(s)
         first_product(2)
         first_product(3)
-        for j in range(PACK):
-            widen_z(2, j, "scalar")
+        widen_z(1, 0, "scalar")
+        widen_z(1, 1, "scalar")
         for i in range(4, 8):
             turn_x(i)
         for i in range(4, 8):
             copy_x(i)
-        widen_z(1, PACK - 1, "vector")
-        group_z(1, "gpsimd", 0, GS)
-        for s in range(4):
-            residual(s)
-        group_z(1, "vector", GS, 8)
+
+        widen_z(0, 3, "vector", Z_COLS, Q)
+        group_z(1, "gpsimd", 0, GPSIMD_COLS)
+        residuals(0)
+        group_z(1, "vector", GPSIMD_COLS, Z_COLS)
         for s in range(4, 8):
-            y_minus_b(s)
-            scale_w(s)
-        for s in range(4, 7):
-            quantize_x(s)
+            make_cw(s)
+        for i in (4, 5, 6):
+            quantize_x(i)
         quantize_z(1)
         quantize_x(7)
         for s in range(4, 8):
             first_product(s)
-        for s in range(4):
+        for s in range(0, 4):
             clip(s)
-        group_t(0, "gpsimd", 0, GS * 64)
+
+        group_t(0, "gpsimd", 0, GPSIMD_COLS)
+        residuals(1)
+        group_t(0, "vector", GPSIMD_COLS, BANK)
+        widen_z(1, 2, "scalar")
+        widen_z(1, 3, "scalar")
+        group_z(2, "scalar", 0, SCALAR_COLS)
+        for s in range(8, 12):
+            make_cw(s)
+        for s in range(8, 12):
+            first_product(s)
+        group_z(2, "vector", SCALAR_COLS, Z_COLS)
+        quantize_t(0)
         for s in range(4, 8):
-            residual(s)
-        group_t(0, "vector", GS * 64, BANK)
-        group_z(2, "scalar")
-        for j in range(PACK):
-            widen_z(3, j, "scalar")
-        for s in range(8, 12):
-            y_minus_b(s)
-            scale_w(s)
-        for s in range(8, 12):
+            clip(s)
+
+        group_t(1, "gpsimd", 0, GPSIMD_COLS)
+        residuals(2)
+        group_t(1, "vector", GPSIMD_COLS, BANK)
+        group_z(3, "scalar")
+        make_cw(12)
+        make_cw(13)
+        for s in range(12, 16):
             first_product(s)
         quantize_z(2)
-        quantize_t(0, 0, BANK)
-        for s in range(4, 8):
+        quantize_t(1)
+        for k in (0, 1):
+            second_product(0, k, 1, side_bank(), "scalar")
+            make_cw(14 + k)
+        for s in (8, 9, 10):
             clip(s)
-        group_t(1, "gpsimd", 0, GS * 64)
-        for s in range(8, 12):
-            residual(s)
-        group_t(1, "vector", GS * 64, BANK)
-        group_z(3, "scalar")
-        for s in range(12, 16):
-            y_minus_b(s)
-            scale_w(s)
-        for s in range(12, 16):
-            first_product(s)
-        clip(8)
-        quantize_t(1, 0, BANK)
-        clip(9)
-        clip(10)
         quantize_z(3)
         clip(11)
-        group_t(2, "gpsimd", 0, GS * 64)
-        for s in range(12, 16):
-            residual(s)
-        group_t(2, "vector", GS * 64, BANK)
-        for i in range(8):
-            second_product(0, i)
-            store_bank(0, i)
+
+        group_t(2, "gpsimd", 0, GPSIMD_COLS)
+        residuals(3)
+        for k in range(2, Q // P):
+            second_product(0, k, 1, side_bank(), "scalar")
+        group_t(2, "vector", GPSIMD_COLS, BANK)
         clip(12)
-        quantize_t(2, 0, BANK)
-        clip(13)
-        clip(14)
-        group_t(3, "vector", 0, BANK // 2)
-        clip(15)
-        quantize_t(3, 0, BANK // 2)
-        group_t(3, "vector", BANK // 2, BANK)
-        for i in range(4):
-            second_product(1, i)
-            store_bank(1, i)
-        last = len(CHUNKS) - 1
-        w = CHUNKS[last][1]
+        quantize_t(2)
+        for s in (13, 14, 15):
+            clip(s)
+
+        halves = ((0, BANK // 2), (BANK // 2, BANK))
+        for lo, hi in halves:
+            group_t(3, "vector", lo, hi)
+        for lo, hi in halves:
+            quantize_t(3, lo, hi)
+        for k in range(0, Q // P, 2):
+            second_product(1, k, 2, side_bank(), "scalar")
         for k in range(Q // P):
-            out_bank[last, k] = bank(ACC_BANKS[k]) if k < len(ACC_BANKS) else side_bank()
-            second_pass(last, k, 0, out_bank[last, k][:, :w])
-        quantize_t(3, BANK // 2, BANK)
-        for k in range(Q // P):
-            second_pass(last, k, 1, out_bank[last, k][:, :w])
-            store(last, out_bank[last, k][:, :w], k, 1, "scalar" if k % 2 == 1 else "vector")
+            dst = bank(ACC_BANKS[k]) if k < len(ACC_BANKS) else side_bank()
+            second_product(2, k, 1, dst, "vector" if k % 2 == 0 else "scalar")

@@ -117,9 +117,9 @@ def tile_iv4rechubermomentmatrix_w4_kernel(tc, x, m_words, m_scales, b, y, c, z_
         nc.scalar.dma_start(out=zs[:], in_=z_scale.rearrange("(g p j) o -> p g (j o)", p=P, j=PACK))
         load_x(0)
         nc.scalar.dma_start(out=c16[:], in_=c.rearrange("(g p j) -> p g j", p=P, j=PACK))
+        nc.sync.dma_start(out=b_row[0:1, :], in_=b.rearrange("(o e) -> o e", o=1))
         load_z(1)
         load_x(1)
-        nc.scalar.dma_start(out=b_row[0:1, :], in_=b.rearrange("(o e) -> o e", o=1))
         for quad in range(4):
             nc.sync.dma_start(
                 out=m_scale[32 * quad : 32 * quad + 4].bitcast(I32),
@@ -350,13 +350,14 @@ def tile_iv4rechubermomentmatrix_w4_kernel(tc, x, m_words, m_scales, b, y, c, z_
 
         widen_z(0, 0, "vector")
         widen_z(0, 1, "scalar")
-        spread_b()
         nc.vector.tensor_copy(out=c32[:], in_=c16[:])
         nc.vector.scalar_tensor_tensor(out=c_hi[:], in0=c16[:], scalar=-1.0, in1=c16[:], op0=ALU.mult, op1=ALU.max)
         nc.vector.scalar_tensor_tensor(out=c_lo[:], in0=c16[:], scalar=-1.0, in1=c16[:], op0=ALU.mult, op1=ALU.min)
-        for i in (0, 1):
-            turn_x(i)
-            copy_x(i)
+        turn_x(0)
+        copy_x(0)
+        spread_b()
+        turn_x(1)
+        copy_x(1)
         widen_z(0, 2, "vector")
         widen_z(0, 3, "vector", 0, Z_COLS)
         quantize_x(0)

import math
from contextlib import ExitStack

import concourse.mybir as mybir
from concourse.masks import make_identity

B, D, E, Q = 1024, 1024, 1024, 1024
FLOPS = 2 * B * D * E + 2 * B * Q * E

F32 = mybir.dt.float32
BF16 = mybir.dt.bfloat16
I32 = mybir.dt.int32
U32 = mybir.dt.uint32
U8 = mybir.dt.uint8
FP8 = mybir.dt.float8_e4m3fn
FP8X4 = mybir.dt.float8_e4m3fn_x4
FP4X4 = mybir.dt.float4_e2m1fn_x4
ALU = mybir.AluOpType
COPY = mybir.ActivationFunctionType.Copy

P = 128
PACK = 4
PASSES = 2
BANK = 512
BATCH = 4
CHUNKS = ((0, 512), (512, 256), (768, 256))
Z_COLS = 512
RUN = 4
GPSIMD_COLS = 384
SCALAR_COLS = 384
OUT_SCALE = 1.0 / math.sqrt(B)

ACC_BANKS = (2, 3, 6, 7)
SIDE_BANKS = (0, 1, 4, 5)


def tile_iv4rechubermomentmatrix_w4_kernel(tc, x, m_words, m_scales, b, y, c, z_bytes, z_scale, out):
    nc = tc.nc

    steps = []
    for ch, (e0, width) in enumerate(CHUNKS):
        per_bank = BANK // width
        for g in range(PASSES):
            for j0 in range(0, PACK, per_bank):
                steps.append((ch, g, range(j0, j0 + per_bank)))
    z_pieces = [(g, h) for g in range(PASSES) for h in range(Q // Z_COLS)]

    x_rows = x.rearrange("(g p j) d -> g j p d", p=P, j=PACK)
    y_rows = y.rearrange("(g p j) e -> g p j e", p=P, j=PACK)
    z_rows = z_bytes.rearrange("(g p j) q -> g p j q", p=P, j=PACK)
    out_rows = out.rearrange("(k p) e -> p k e", p=P)

    with ExitStack() as ctx:
        keep = ctx.enter_context(tc.tile_pool(name="keep", bufs=1))
        ring = ctx.enter_context(tc.tile_pool(name="ring", bufs=BATCH))
        deep = ctx.enter_context(tc.tile_pool(name="deep", bufs=2 * BATCH))
        psum = ctx.enter_context(tc.psum_pool(name="psum", bufs=1))
        ctx.enter_context(tc.manual_schedule())

        def kept(name, shape, dtype):
            return keep.tile(shape, dtype, name=name, align_bytes=64)

        def bank(index):
            return psum.tile([P, BANK], F32, name="bank%d" % index)

        side_taken = []

        def side_bank():
            side_taken.append(SIDE_BANKS[len(side_taken) % len(SIDE_BANKS)])
            return bank(side_taken[-1])

        m_scale = kept("m_scale", [P, PASSES, E], U8)
        b_row = kept("b_row", [P, E], BF16)
        ident32 = kept("ident32", [P, P], F32)
        ident16 = kept("ident16", [P, P], BF16)
        minus_ones = kept("minus_ones", [P, P], BF16)
        zs = kept("zs", [P, PASSES, PACK], F32)
        c16 = kept("c16", [P, PASSES, PACK], BF16)
        c32 = kept("c32", [P, PASSES, PACK], F32)
        c_hi = kept("c_hi", [P, PASSES, PACK], F32)
        c_lo = kept("c_lo", [P, PASSES, PACK], F32)
        minus_b = kept("minus_b", [P, BANK], F32)

        x_in = [kept("x_in%d" % i, [P, D], BF16) for i in range(PASSES * PACK)]
        y_in = [kept("y_in%d" % i, [P, 2 * BANK], BF16) for i in range(len(steps) // 2)]
        z_in = [kept("z_in%d" % i, [P, 2, Q], U8) for i in range(2 * PASSES)]
        m_in = [kept("m_in%d" % ch, [P, PASSES, 2 * w], U8) for ch, (e0, w) in enumerate(CHUNKS)]

        def load_x(i):
            nc.sync.dma_start(out=x_in[i][:], in_=x_rows[i // PACK, i % PACK])

        def load_y(i):
            ch, g, js = steps[2 * i]
            e0, w = CHUNKS[ch]
            planes = 2 * BANK // w
            nc.sync.dma_start(
                out=y_in[i][:].rearrange("p (j e) -> p j e", j=planes),
                in_=y_rows[g][:, js[0] : js[0] + planes, e0 : e0 + w],
            )

        def load_z(i):
            nc.sync.dma_start(out=z_in[i][:], in_=z_rows[i // 2][:, 2 * (i % 2) : 2 * (i % 2) + 2, :])

        def load_m(ch):
            e0, w = CHUNKS[ch]
            nc.sync.dma_start(
                out=m_in[ch][:].bitcast(I32),
                in_=m_words.rearrange("g p n -> p g n")[:, :, 2 * e0 : 2 * (e0 + w)].bitcast(I32),
            )

        nc.vector.memset(b_row[:].bitcast(I32), 0)
        nc.vector.memset(m_scale[:].rearrange("p g n -> p (g n)").bitcast(I32), 0)
        make_identity(nc, ident32[:])
        nc.gpsimd.memset(minus_ones[:], -1.0)

        load_z(0)
        nc.scalar.dma_start(out=zs[:], in_=z_scale.rearrange("(g p j) o -> p g (j o)", p=P, j=PACK))
        load_x(0)
        nc.scalar.dma_start(out=c16[:], in_=c.rearrange("(g p j) -> p g j", p=P, j=PACK))
        nc.sync.dma_start(out=b_row[0:1, :], in_=b.rearrange("(o e) -> o e", o=1))
        load_z(1)
        load_x(1)
        for quad in range(4):
            nc.sync.dma_start(
                out=m_scale[32 * quad : 32 * quad + 4].bitcast(I32),
                in_=m_scales[:, 4 * quad : 4 * quad + 4, :].rearrange("g r n -> r g n").bitcast(I32),
            )
        load_m(0)
        load_y(0)
        load_x(2)
        load_x(3)
        load_y(1)
        load_z(2)
        for i in range(PACK, 2 * PACK):
            load_x(i)
        load_y(2)
        load_y(3)
        load_z(3)
        for ch in (1, 2):
            load_m(ch)
            load_y(2 + 2 * ch)
            load_y(3 + 2 * ch)
        nc.scalar.copy(out=ident16[:], in_=ident32[:])

        x_turned, x_grouped, x_q = {}, {}, {}
        z_wide, z_grouped, z_q = {}, {}, {}
        w_bank, minus_cb, cw, acc, unclipped = {}, {}, {}, {}, {}
        t_planes, t_grouped, t_q = {}, {}, {}

        def quantize(name, grouped, cols):
            codes = kept(name + "_codes", [P, cols], U32)
            scales = kept(name + "_scales", [P, cols], U8)
            nc.vector.quantize_mx(out=codes[:].bitcast(FP8X4), scales=scales[:], in_=grouped[:])
            return codes, scales

        def interleave(engine, grouped, planes):
            if engine == "gpsimd":
                nc.gpsimd.tensor_scalar(
                    out=grouped.rearrange("p (n j) -> p n j", j=PACK),
                    in0=planes.rearrange("p j n -> p n j"),
                    scalar1=1.0,
                    scalar2=0.0,
                    op0=ALU.mult,
                    op1=ALU.add,
                )
                return
            dst = grouped.rearrange("p (n i j) -> p n j i", i=RUN, j=PACK)
            src = planes.rearrange("p j (n i) -> p n j i", i=RUN)
            if engine == "vector":
                nc.vector.tensor_copy(out=dst, in_=src)
            else:
                nc.scalar.copy(out=dst, in_=src)

        def turn_x(i):
            x_turned[i] = side_bank()
            words = x_in[i][:].bitcast(F32)
            for kp in range(PASSES):
                for u in range(2):
                    col = (2 * kp + u) * P
                    nc.tensor.transpose(
                        x_turned[i][:, col : col + P], words[:, 2 * P * kp + u : 2 * P * (kp + 1) : 2], ident32[:]
                    )

        def copy_x(i):
            x_grouped[i] = ring.tile([P, D], BF16, name="x_grouped", align_bytes=64)
            nc.scalar.copy(
                out=x_grouped[i][:].bitcast(F32).rearrange("p (k r u) -> p k r u", k=PASSES, u=2),
                in_=x_turned[i][:].rearrange("p (k u r) -> p k r u", k=PASSES, u=2),
            )

        def quantize_x(i):
            x_q[i] = quantize("x%d" % i, x_grouped[i], PASSES * P)

        def widen_z(g, j, engine, lo=0, hi=Q):
            if g not in z_wide:
                z_wide[g] = kept("z_wide%d" % g, [P, PACK, Q], BF16)
            src = z_in[2 * g + j // 2][:, j % 2, lo:hi].bitcast(FP8)
            dst = z_wide[g][:, j, lo:hi]
            if engine == "vector":
                nc.vector.tensor_scalar(out=dst, in0=src, scalar1=zs[:, g, j : j + 1], scalar2=None, op0=ALU.mult)
            else:
                nc.scalar.activation(out=dst, in_=src, func=COPY, scale=zs[:, g, j : j + 1])

        def group_z(i, engine, lo=0, hi=Z_COLS):
            g, h = z_pieces[i]
            if i not in z_grouped:
                z_grouped[i] = kept("z_grouped%d" % i, [P, PACK * Z_COLS], BF16)
            q0 = h * Z_COLS
            interleave(engine, z_grouped[i][:, PACK * lo : PACK * hi], z_wide[g][:, :, q0 + lo : q0 + hi])

        def quantize_z(i):
            z_q[z_pieces[i]] = quantize("z%d" % i, z_grouped[i], Z_COLS)

        def y_plane(s, jj):
            w = CHUNKS[steps[s][0]][1]
            col = (s % 2) * BANK + jj * w
            return y_in[s // 2][:, col : col + w]

        def spread_b():
            spread = side_bank()
            nc.tensor.matmul(spread[:], lhsT=minus_ones[:], rhs=b_row[:, :BANK], start=True, stop=True)
            nc.scalar.copy(out=minus_b[:], in_=spread[:])

        def scale_b(s):
            ch, g, js = steps[s]
            minus_cb[s] = ring.tile([P, BANK], F32, name="minus_cb", align_bytes=64)
            nc.scalar.activation(out=minus_cb[s][:], in_=minus_b[:], func=COPY, scale=c32[:, g, js[0] : js[0] + 1])

        def add_cy(s):
            ch, g, js = steps[s]
            cw[s] = ring.tile([P, BANK], F32, name="cw_first", align_bytes=64)
            nc.vector.scalar_tensor_tensor(
                out=cw[s][:],
                in0=y_plane(s, 0),
                scalar=c32[:, g, js[0] : js[0] + 1],
                in1=minus_cb[s][:],
                op0=ALU.mult,
                op1=ALU.add,
            )

        def make_cw(s):
            ch, g, js = steps[s]
            e0, w = CHUNKS[ch]
            w_bank[s] = side_bank()
            for jj in range(len(js)):
                dst = w_bank[s][:, jj * w : (jj + 1) * w]
                nc.tensor.matmul(dst, lhsT=minus_ones[:], rhs=b_row[:, e0 : e0 + w], start=True, stop=False)
                nc.tensor.matmul(dst, lhsT=ident16[:], rhs=y_plane(s, jj), start=False, stop=True)
            cw[s] = deep.tile([P, BANK], F32, name="cw", align_bytes=64)
            for jj, j in enumerate(js):
                cols = slice(jj * w, (jj + 1) * w)
                nc.scalar.activation(out=cw[s][:, cols], in_=w_bank[s][:, cols], func=COPY, scale=c32[:, g, j : j + 1])

        def first_product(s):
            ch, g, js = steps[s]
            e0, w = CHUNKS[ch]
            n = w if w == BANK else P
            acc[s] = bank(ACC_BANKS[s % BATCH])
            for jj, j in enumerate(js):
                codes, scales = x_q[g * PACK + j]
                for n0 in range(0, w, n):
                    for kp in range(PASSES):
                        nc.tensor.matmul_mx(
                            out=acc[s][:, jj * w + n0 : jj * w + n0 + n],
                            lhsT=codes[:, kp * P : (kp + 1) * P].bitcast(FP8X4),
                            lhsT_scale=scales[:, kp * P : (kp + 1) * P],
                            rhs=m_in[ch][:, kp, 2 * n0 : 2 * (n0 + n)].bitcast(FP4X4),
                            rhs_scale=m_scale[:, kp, e0 + n0 : e0 + n0 + n],
                            start=(kp == 0),
                            stop=(kp == PASSES - 1),
                        )

        def residuals(batch):
            for s in range(BATCH * batch, BATCH * (batch + 1)):
                ch, g, js = steps[s]
                w = CHUNKS[ch][1]
                unclipped[s] = ring.tile([P, BANK], F32, name="unclipped", align_bytes=64)
                for jj, j in enumerate(js):
                    cols = slice(jj * w, (jj + 1) * w)
                    nc.vector.scalar_tensor_tensor(
                        out=unclipped[s][:, cols],
                        in0=acc[s][:, cols],
                        scalar=c32[:, g, j : j + 1],
                        in1=cw[s][:, cols],
                        op0=ALU.mult,
                        op1=ALU.subtract,
                    )

        def clip(s):
            ch, g, js = steps[s]
            w = CHUNKS[ch][1]
            batch = s // BATCH
            if batch not in t_planes:
                t_planes[batch] = kept("t_planes%d" % batch, [P, PACK, BANK], BF16)
            col = g * w % BANK
            for jj, j in enumerate(js):
                nc.vector.tensor_scalar(
                    out=t_planes[batch][:, j, col : col + w],
                    in0=unclipped[s][:, jj * w : (jj + 1) * w],
                    scalar1=c_hi[:, g, j : j + 1],
                    scalar2=c_lo[:, g, j : j + 1],
                    op0=ALU.min,
                    op1=ALU.max,
                )

        def group_t(batch, engine, lo, hi):
            if batch not in t_grouped:
                t_grouped[batch] = kept("t_grouped%d" % batch, [P, PACK * BANK], BF16)
            interleave(engine, t_grouped[batch][:, PACK * lo : PACK * hi], t_planes[batch][:, :, lo:hi])

        def quantize_t(batch, lo=0, hi=BANK):
            if batch not in t_q:
                t_q[batch] = (kept("t_codes%d" % batch, [P, BANK], U32), kept("t_scales%d" % batch, [P, BANK], U8))
            codes, scales = t_q[batch]
            nc.vector.quantize_mx(
                out=codes[:, lo:hi].bitcast(FP8X4),
                scales=scales[:, lo:hi],
                in_=t_grouped[batch][:, PACK * lo : PACK * hi],
            )

        def second_product(ch, k0, blocks, dst, engine):
            e0, w = CHUNKS[ch]
            for kk in range(blocks):
                q0 = (k0 + kk) * P
                for g in range(PASSES):
                    z_codes, z_scales = z_q[g, q0 // Z_COLS]
                    t_codes, t_scales = t_q[g if ch == 0 else ch + 1]
                    z_cols = slice(q0 % Z_COLS, q0 % Z_COLS + P)
                    t_cols = slice(g * w % BANK, g * w % BANK + w)
                    nc.tensor.matmul_mx(
                        out=dst[:, kk * w : (kk + 1) * w],
                        lhsT=z_codes[:, z_cols].bitcast(FP8X4),
                        lhsT_scale=z_scales[:, z_cols],
                        rhs=t_codes[:, t_cols].bitcast(FP8X4),
                        rhs_scale=t_scales[:, t_cols],
                        start=(g == 0),
                        stop=(g == PASSES - 1),
                    )
            result = kept("result%d_%d" % (ch, k0), [P, blocks * w], F32)
            if engine == "vector":
                nc.vector.tensor_scalar(
                    out=result[:], in0=dst[:, : blocks * w], scalar1=OUT_SCALE, scalar2=None, op0=ALU.mult
                )
            else:
                nc.scalar.activation(out=result[:], in_=dst[:, : blocks * w], func=COPY, scale=OUT_SCALE)
            nc.sync.dma_start(
                out=out_rows[:, k0 : k0 + blocks, e0 : e0 + w], in_=result[:].rearrange("p (k e) -> p k e", k=blocks)
            )


        widen_z(0, 0, "vector")
        widen_z(0, 1, "scalar")
        nc.vector.tensor_copy(out=c32[:], in_=c16[:])
        nc.vector.scalar_tensor_tensor(out=c_hi[:], in0=c16[:], scalar=-1.0, in1=c16[:], op0=ALU.mult, op1=ALU.max)
        nc.vector.scalar_tensor_tensor(out=c_lo[:], in0=c16[:], scalar=-1.0, in1=c16[:], op0=ALU.mult, op1=ALU.min)
        turn_x(0)
        copy_x(0)
        spread_b()
        turn_x(1)
        copy_x(1)
        widen_z(0, 2, "vector")
        widen_z(0, 3, "vector", 0, Z_COLS)
        quantize_x(0)
        group_z(0, "vector")
        quantize_x(1)
        quantize_z(0)
        for s in (0, 1, 2):
            scale_b(s)
        first_product(0)
        for i in (2, 3):
            turn_x(i)
            copy_x(i)
        first_product(1)
        scale_b(3)
        add_cy(0)
        add_cy(1)
        for s in (2, 3):
            quantize_x(s)
            add_cy(s)
        first_product(2)
        first_product(3)
        widen_z(1, 0, "scalar")
        widen_z(1, 1, "scalar")
        for i in range(4, 8):
            turn_x(i)
        for i in range(4, 8):
            copy_x(i)

        widen_z(0, 3, "vector", Z_COLS, Q)
        group_z(1, "gpsimd", 0, GPSIMD_COLS)
        residuals(0)
        group_z(1, "vector", GPSIMD_COLS, Z_COLS)
        for s in range(4, 8):
            make_cw(s)
        for i in (4, 5, 6):
            quantize_x(i)
        quantize_z(1)
        quantize_x(7)
        for s in range(4, 8):
            first_product(s)
        for s in range(0, 4):
            clip(s)

        group_t(0, "gpsimd", 0, GPSIMD_COLS)
        residuals(1)
        group_t(0, "vector", GPSIMD_COLS, BANK)
        widen_z(1, 2, "scalar")
        widen_z(1, 3, "scalar")
        group_z(2, "scalar", 0, SCALAR_COLS)
        for s in range(8, 12):
            make_cw(s)
        for s in range(8, 12):
            first_product(s)
        group_z(2, "vector", SCALAR_COLS, Z_COLS)
        quantize_t(0)
        for s in range(4, 8):
            clip(s)

        group_t(1, "gpsimd", 0, GPSIMD_COLS)
        residuals(2)
        group_t(1, "vector", GPSIMD_COLS, BANK)
        group_z(3, "scalar")
        make_cw(12)
        make_cw(13)
        for s in range(12, 16):
            first_product(s)
        quantize_z(2)
        quantize_t(1)
        for k in (0, 1):
            second_product(0, k, 1, side_bank(), "scalar")
            make_cw(14 + k)
        for s in (8, 9, 10):
            clip(s)
        quantize_z(3)
        clip(11)

        group_t(2, "gpsimd", 0, GPSIMD_COLS)
        residuals(3)
        for k in range(2, Q // P):
            second_product(0, k, 1, side_bank(), "scalar")
        group_t(2, "vector", GPSIMD_COLS, BANK)
        clip(12)
        quantize_t(2)
        for s in (13, 14, 15):
            clip(s)

        halves = ((0, BANK // 2), (BANK // 2, BANK))
        for lo, hi in halves:
            group_t(3, "vector", lo, hi)
        for lo, hi in halves:
            quantize_t(3, lo, hi)
        for k in range(0, Q // P, 2):
            second_product(1, k, 2, side_bank(), "scalar")
        for k in range(Q // P):
            dst = bank(ACC_BANKS[k]) if k < len(ACC_BANKS) else side_bank()
            second_product(2, k, 1, dst, "vector" if k % 2 == 0 else "scalar")
